import numpy as np, ml_dtypes
CORES = [16,18,20,22]
N = 4
BF = ml_dtypes.bfloat16
def gentries(a):
    return np.ascontiguousarray(a.reshape(8, 16, -1).transpose(0, 2, 1)).reshape(8, -1)
def gtable(e):
    e = np.asarray(e); return np.ascontiguousarray(e.reshape(8, -1, 16).transpose(0, 2, 1)).reshape(128, -1).astype(np.int32)
F, A, GI, D, E, RO = 3072, 3072, 2, 1024, 128, 3
L = GI + RO - 1
R = 16 // N
NE = [F] + [A] * GI + [D] * (RO - 1)
ST = [sum(NE[:e]) + e * E for e in range(L + 1)]
PO = [0] + [sum(NE[1:e]) for e in range(1, L + 1)]
W = ST[L] + NE[L]; M = GI * A + (RO - 1) * D
def cols(e):
    o = np.concatenate([np.arange(ST[k], ST[k] + NE[k]) for k in range(e)]); g = np.concatenate([np.arange(ST[k] + NE[k], ST[k] + NE[k] + E) for k in range(e)])
    return o, g
def parts(rng):
    h = rng.integers(0, 65536, (N, 8, 16, F)); t = rng.integers(0, 65536, (8, 16))
    s = np.zeros((N, 8, GI * A), np.int64); d = np.zeros((N, 8, M), np.int64); m = np.zeros((N, 8, L * E), np.int64)
    for e in range(1, L + 1):
        o, g = cols(e); p, n = PO[e], NE[e]
        if e <= GI: s[:, :, p:p + n] = rng.choice(o, (N, 8, n))
        d[:, :, p:p + n] = np.where(rng.random((N, 8, n)) < 0.25, rng.choice(g, (N, 8, n)), rng.choice(o, (N, 8, n)))
    for e in range(L): m[:, :, e * E:(e + 1) * E] = rng.integers(0, NE[e], (N, 8, E))
    return h, t, s, d, m
def pack(h, t, s, d, m):
    return {"trait": np.ascontiguousarray(h.reshape(N, 128, F)).astype(np.int32), "aim0": np.tile(t.reshape(1, 128, 1), (N, 1, 1)).astype(np.int32),
            "sire": np.stack([gtable(a) for a in s]), "dam": np.stack([gtable(a) for a in d]), "mg": np.stack([gtable(a) for a in m])}
def setup_inputs(rng):
    return pack(*parts(rng))
def plant(rng, h, t, s, d, m, g, j, up):
    t[g] = rng.integers(0, 1000, 16); low = rng.integers(1000, 5000, 14)
    for q in range(N):
        c = 1 + rng.permutation(F - 1); x, y, z, a0, a1, b = [int(v) for v in c[:6]]; rest = c[6:]
        w = rng.integers(20000, 55000, (16, F)); w[0] = rng.integers(60000, 65536, F); w[1] = rng.integers(2000, 40000, F)
        w[:2, [x, y, z, b]] = rng.integers(2000, 40000, (2, 4)); w[1, b] = rng.integers(60000, 65536); w[0, x] = 1000; w[1, y] = 1000
        w[2:, y] = rng.integers(1000, 5000, 14) + 5000 * (q % 2); w[2:, x] = w[2:, y] + 40000; w[2:, z] = rng.integers(60000, 65536, 14)
        w[2:, a0] = low; w[2:, a1] = low + up; w[2:, b] = low + 40000; h[q, g] = w
        col = a1
        for e in range(1, GI):
            k = int(rng.integers(0, A)); s[q, g, PO[e] + k] = a0; d[q, g, PO[e] + k] = col; col = ST[e] + k
        o = rng.choice(rest, A); k = rng.permutation(A)[:4]; o[k[:3]] = (x, y, z); p = PO[GI]
        s[q, g, p:p + A] = o; d[q, g, p:p + A] = o; s[q, g, p + k[3]] = a0; d[q, g, p + k[3]] = col
        v = rng.choice(rest, D); v[int(rng.integers(1, D - 1))] = ST[GI] + k[3]; v[j] = b
        d[q, g, PO[GI + 1]:PO[GI + 1] + D] = v; m[q, g, (GI + 1) * E] = j
def setup_inputs_ends(rng):
    h, t, s, d, m = parts(rng); t = rng.choice(np.array([0, 1, 32767, 65534, 65535]), (8, 16))
    for e in range(1, L + 1):
        o, g = cols(e); p, n = PO[e], NE[e]
        if e <= GI: s[:, 4:, p:p + n] = rng.choice(np.array([0, F - 1, o[-1]]), (N, 4, n))
        d[:, 4:, p:p + n] = rng.choice(np.array([0, F - 1, F, F + E - 1, o[-1], g[-1]]), (N, 4, n))
    for e in range(L): m[:, 4:, e * E:(e + 1) * E] = rng.choice(np.array([0, NE[e] - 1]), (N, 4, E))
    h[:, :4, :, 7] = t[:4]; h[:, :4, :, 9] = np.where(t[:4] < 32768, 65535, 0); a, z = (GI - 1) * A, GI * A - 1
    for g in range(4):
        x, y = (7, 9) if g < 2 else (9, 7)
        s[:, g, z] = x; d[:, g, z] = x; s[:, g, a] = y; d[:, g, a] = y
    plant(rng, h, t, s, d, m, 6, D - 1, 1); plant(rng, h, t, s, d, m, 7, 0, 0)
    return pack(h, t, s, d, m)
def setup_inputs_ghosts(rng):
    h, t, s, d, m = parts(rng)
    for e in range(1, L + 1):
        o, g = cols(e); p, n = PO[e], NE[e]
        d[:, 0::2, p:p + n] = rng.choice(g, (N, 4, n)); d[:, 1, p:p + n] = rng.choice(o, (N, n))
        d[:, 6, p:p + n] = rng.integers(ST[e] - E, ST[e], (N, n))
        if e > GI: d[:, 3, p:p + n] = rng.integers(ST[e - 1], ST[e - 1] + NE[e - 1], (N, n))
    d[:, 3, :GI * A] = s[:, 3]
    for e in range(L):
        m[:, 5, e * E:(e + 1) * E] = rng.integers(0, NE[e], (N, 1)); m[:, 7, e * E:(e + 1) * E] = NE[e] - 1
    return pack(h, t, s, d, m)
def setup_inputs_lines(rng):
    h, t, s, d, m = parts(rng); t[5] = rng.integers(0, 65536)
    for e in range(1, L + 1):
        p, n = PO[e], NE[e]; lo, hi = ST[e - 1], ST[e - 1] + NE[e - 1]
        if e <= GI:
            s[:, 0:2, p:p + n] = rng.integers(lo, hi, (N, 2, n)); s[:, 2:4, p:p + n] = rng.integers(0, F, (N, 2, n))
            s[:, 4, p:p + n] = np.where(rng.random((N, n)) < 0.9, rng.integers(lo, hi, (N, 1)), rng.integers(lo, hi, (N, n)))
            d[:, 7, p:p + n] = rng.integers(1, ST[e], (N, 1))
        d[:, 0::4, p:p + n] = rng.integers(lo, hi, (N, 2, n)); d[:, 1::4, p:p + n] = rng.integers(0, F, (N, 2, n))
        for g, k in ((2, 1), (3, 2), (6, 3)):
            y = min(k, e - 1); d[:, g, p:p + n] = rng.integers(ST[y], ST[y] + NE[y], (N, n))
    return pack(h, t, s, d, m)
def setup_inputs_spread(rng):
    h, t, s, d, m = parts(rng)
    h = np.minimum((np.exp2(17 * rng.random((N, 8, 1, F))) * rng.random((N, 8, 16, F))).astype(np.int64), 65535)
    t = np.minimum(np.exp2(16 * rng.random((8, 16))).astype(np.int64), 65535)
    for e in range(1, L + 1):
        o, g = cols(e); p, n = PO[e], NE[e]; o = rng.permutation(o); g = rng.permutation(g)
        if e <= GI: s[:, :, p:p + n] = o[(len(o) * rng.random((N, 8, n)) ** 4).astype(np.int64)]
        d[:, :, p:p + n] = np.where(rng.random((N, 8, n)) < 0.5, g[(len(g) * rng.random((N, 8, n)) ** 3).astype(np.int64)], o[(len(o) * rng.random((N, 8, n)) ** 3).astype(np.int64)])
    for e in range(L): m[:, :, e * E:(e + 1) * E] = (NE[e] * rng.random((N, 8, E)) ** 3).astype(np.int64)
    return pack(h, t, s, d, m)
def setup_inputs_ties(rng):
    h, t, s, d, m = parts(rng)
    h[:, 0] = 5; t[0] = rng.choice(np.array([3, 4, 1000, 60000]), 16)
    t[0, 14] = 5; h[:, 0, 14, 0] = 60000; t[0, 15] = 0; h[:, 0, 15] = 65535
    s[:, 0] = np.where(s[:, 0] == 0, 1, s[:, 0]); d[:, 0] = np.where(d[:, 0] == 0, 1, d[:, 0]); m[:, 0, :E] = np.where(m[:, 0, :E] == 0, 1, m[:, 0, :E])
    h[:, 1:3] = rng.choice(np.array([0, 1, 32768, 65535]), (N, 2, 16, F)); t[1:3] = rng.choice(np.array([0, 1, 32768, 65535]), (2, 16))
    h[:, 3:5, 8:] = h[:, 3:5, :8]; t[3:5, 8:] = t[3:5, :8]
    h[:, 5] = 65535 * rng.integers(0, 2, (N, 16, F)); t[5] = 65535 * rng.integers(0, 2, 16)
    h[:, 6] = h[:, 6][:, :, np.arange(F) % 16]
    t[7] = 32768; h[:, 7] = 32768 + 20000 * (2 * rng.integers(0, 2, (N, 16, F)) - 1)
    return pack(h, t, s, d, m)
def check_inputs(d):
    bad = []
    for k in ("trait", "aim0"):
        if np.min(d[k]) < 0 or np.max(d[k]) > 65535: bad.append("range of " + k)
    if np.any(d["aim0"] != d["aim0"][:1]): bad.append("aim0 alike on all ranks")
    s = np.stack([gentries(a) for a in d["sire"]]); w = np.stack([gentries(a) for a in d["dam"]]); m = np.stack([gentries(a) for a in d["mg"]])
    for e in range(1, GI + 1):
        if not np.all(np.isin(s[:, :, PO[e]:PO[e] + NE[e]], cols(e)[0])): bad.append("sires of generation " + str(e))
    for e in range(1, L + 1):
        x = w[:, :, PO[e]:PO[e] + NE[e]]
        if np.min(x) < 0 or np.max(x) >= ST[e]: bad.append("dams of generation " + str(e))
    for e in range(L):
        x = m[:, :, e * E:(e + 1) * E]
        if np.min(x) < 0 or np.max(x) >= NE[e]: bad.append("emigrants of generation " + str(e))
    return bad
def pick(w, ix):
    return np.take_along_axis(w, ix[:, :, None, :], 3)
def reference(trait, aim0, sire, dam, mg):
    h = trait.astype(np.int64).reshape(N, 8, 16, F); t = aim0.astype(np.int64).reshape(N, 8, 16, 1)
    sl = np.zeros((N, 8, M), np.int64); sl[:, :, :GI * A] = np.stack([gentries(a) for a in sire])
    dl = np.stack([gentries(a) for a in dam]).astype(np.int64); ml = np.stack([gentries(a) for a in mg]).astype(np.int64)
    top = np.zeros((N, 8, W), np.int64); top[:, :, :F] = np.arange(F)
    for e in range(1, GI + 1): top[:, :, ST[e]:ST[e] + NE[e]] = np.take_along_axis(top, sl[:, :, PO[e]:PO[e] + NE[e]], 2)
    f = np.zeros((N, 8, 16, W)); aims = []
    for rnd in range(1, RO + 1):
        new = GI + rnd - 1
        for e in range(new + 1):
            a, n, p = ST[e], NE[e], PO[e]
            if e == 0: f[:, :, :, :F] = 65535 - np.abs(h - t)
            else: f[:, :, :, a:a + n] = (pick(f, sl[:, :, p:p + n]) + pick(f, dl[:, :, p:p + n])) * 0.5
            if e < L: f[:, :, :, a + n:a + n + E] = np.roll(pick(f[:, :, :, a:a + n], ml[:, :, e * E:(e + 1) * E]), 1, axis=0)
        if rnd == RO: break
        a, n = ST[new], NE[new]; x = f[:, :, :, a:a + n]
        best = a + np.argmax(x, axis=3); least = a + np.argmin(x, axis=3)
        b, p = ST[new + 1], PO[new + 1]
        row = np.argmin(pick(f, dl[:, :, p:p + D]), axis=2)
        sl[:, :, p:p + D] = np.take_along_axis(best, row, 2)
        old = np.take_along_axis(h, np.take_along_axis(top, least, 2)[:, :, :, None], 3)[:, :, :, 0]
        top[:, :, b:b + D] = np.take_along_axis(top, sl[:, :, p:p + D], 2)
        t1 = np.stack([old[m // R, :, m] for m in range(16)], axis=1)
        t = np.tile(t1.reshape(1, 8, 16, 1), (N, 1, 1, 1)); aims.append(t.reshape(N, 128))
    made = np.concatenate([f[:, :, :, ST[e]:ST[e] + NE[e]] for e in range(GI + 1, L + 1)], axis=3)
    return {"yf": made.reshape(N, 128, (RO - 1) * D).astype(np.float32), "ys": np.stack([gtable(a) for a in sl[:, :, GI * A:]]).astype(np.float32), "yt": np.stack(aims, axis=2).astype(np.float32)}

@@ -1,0 +1,566 @@
+from concourse.bass import DstId, RemoteDMATransfer
+from concourse.mybir import AluOpType, AxisListType, ActivationFunctionType
+
+ALU = AluOpType
+AF = ActivationFunctionType
+F32, I32, U16, B16 = "float32", "int32", "uint16", "bfloat16"
+Z0 = 8
+OWN1 = Z0 + 6272
+G1 = Z0 + 6272
+G1X = Z0 + 6400
+G2X = Z0 + 6528
+X3 = Z0 + 6656
+G3X = Z0 + 7680
+TW = Z0 + 7808
+CUT = 1536
+
+
+def _sb(n, d=F32):
+    return ("sbuf", [128, n], d)
+
+
+SCRATCH = {
+    "sireI": _sb(384, I32), "damI": _sb(528, I32), "mgI": _sb(32, I32), "aimI": _sb(1, I32),
+    "trI": _sb(3072, I32), "W": _sb(3152, I32),
+    "y1": _sb(3200), "FH": _sb(3200), "tabA": _sb(TW), "tabB": _sb(TW),
+    "tmp": _sb(3072), "tmp2": _sb(1536), "D2": _sb(2048), "CF": _sb(2304),
+    "T3": _sb(1024), "T4": _sb(1024), "key": _sb(1024), "G3": _sb(1024),
+    "yo": _sb(2048), "sf": _sb(2048), "seg": _sb(1024), "zero": _sb(512),
+    "io": _sb(512), "dmj": _sb(512), "mk": _sb(512), "msc": _sb(512), "junk": _sb(3072, B16),
+    "Y": _sb(143), "Gm": _sb(128), "blk": _sb(128), "bs1": _sb(128), "bd1": _sb(128), "bs2": _sb(128), "bd2": _sb(128),
+    "ident": _sb(128), "ZS": _sb(143), "ZD": _sb(143),
+    "R00": _sb(128, B16), "R01": _sb(128, B16), "R10": _sb(128, B16), "R11": _sb(128, B16),
+    "pI": _sb(8, I32), "cc": _sb(32), "dm": _sb(16), "dmo": _sb(16), "dmh": _sb(16),
+    "sire16": _sb(384, U16), "dam16": _sb(384, U16), "mg16": _sb(32, U16), "ms16": _sb(32, U16),
+    "pos16": _sb(144, U16), "US16": _sb(128, U16), "UD16": _sb(128, U16), "row16": _sb(128, U16), "sm16": _sb(64, U16),
+    "EI": _sb(144, I32), "AI": _sb(144, I32), "EF": _sb(144), "EG": _sb(144),
+    "q1": _sb(128), "pp": _sb(128), "qq": _sb(128), "is2": _sb(128), "xs": _sb(128), "w8": _sb(128), "PS": _sb(128),
+    "k1": _sb(128), "q3": _sb(128), "r1": _sb(128), "r2": _sb(128), "n2": _sb(128), "PD": _sb(128),
+    "lS": _sb(128), "lD": _sb(128), "lS2": _sb(128), "lD2": _sb(128),
+    "gs": _sb(1152), "gt": _sb(768), "ri": _sb(64, I32), "rb": _sb(64, I32), "rbf": _sb(64, B16),
+    "bT": _sb(32), "bR": _sb(32), "bg": _sb(16), "bm": _sb(32), "bsc": _sb(32), "Ub": _sb(16), "ub1": _sb(16), "HB": _sb(16),
+    "cl": _sb(64), "ci": _sb(64, I32), "lk": _sb(128), "land1": _sb(16), "land2": _sb(16),
+    "yso": _sb(128), "yto": _sb(2),
+}
+BANKS = ("pC", "pS", "pD", "pM", "pY", "pA", "pB", "pE")
+for _b in BANKS:
+    SCRATCH[_b] = ("psum", [128, 512], F32)
+SEMAPHORES = ["qV", "qA", "qP", "qG", "sent", "l_sire", "l_sire2", "l_dam0", "l_dam1", "l_dam2", "l_mg", "l_aim",
+              "l_t0", "l_t1", "l_t2", "l_t3", "l_w", "l_w2", "l_tr", "o_ys", "o_yt", "o_f3", "o_f4a", "o_f4b",
+              "a_g0", "a_g11", "a_g12", "a_g13", "a_g21", "a_g22", "a_g23", "a_g32", "a_g33", "a_aim1", "a_aim2"]
+
+
+def rank_program(g, core, T, topo):
+    rank = T.rank_of(core)
+    if rank is None:
+        return
+    N = len(T.cores)
+    nxt = T.cores[(rank + 1) % N]
+    Q = {"V": g.vector, "A": g.scalar, "P": g.tensor, "G": g, "S": g.sync}
+    SEM = {"V": "qV", "A": "qA", "P": "qP", "G": "qG"}
+    cnt = {"V": 0, "A": 0, "P": 0, "G": 0}
+    known = {e: {} for e in Q}
+    recs = {}
+    clocks = {}
+    total = {}
+
+    def need(e, reads, writes, acc=False):
+        req = {}
+        for kind, regs in ((0, reads), (1, writes)):
+            for b, c0, c1 in regs:
+                for o0, o1, ow, sem, val, oe in recs.get(b, []):
+                    if o1 <= c0 or o0 >= c1 or (kind == 0 and not ow) or (oe == e and acc):
+                        continue
+                    req[sem] = max(req.get(sem, 0), val)
+        live = {s: v for s, v in req.items() if known[e].get(s, 0) < v}
+        for s in sorted(live):
+            if any(o != s and clocks.get((o, live[o]), {}).get(s, 0) >= live[s] for o in live):
+                continue
+            Q[e].wait_ge(T.sem[s], live[s])
+        for s, v in live.items():
+            known[e][s] = max(known[e].get(s, 0), v)
+            for o, w in clocks.get((s, v), {}).items():
+                known[e][o] = max(known[e].get(o, 0), w)
+
+    def note(e, reads, writes, sem, val):
+        clocks[(sem, val)] = dict(known[e]) if e in known else {}
+        total[sem] = val
+        for b, c0, c1 in writes:
+            keep = [r for r in recs.get(b, []) if not (c0 <= r[0] and r[1] <= c1)]
+            keep.append((c0, c1, True, sem, val, e))
+            recs[b] = keep
+        for b, c0, c1 in reads:
+            keep = [r for r in recs.get(b, []) if not (not r[2] and r[5] == e and c0 <= r[0] and r[1] <= c1)]
+            keep.append((c0, c1, False, sem, val, e))
+            recs[b] = keep
+
+    def reg(x):
+        return (x[0], 0, 512) if x[0] in BANKS else (x[0], x[1], x[2])
+
+    def ap(x):
+        if len(x) == 4:
+            return T[x[0]][:, x[1]:x[2]:x[3]]
+        return T[x[0]][:, x[1]:x[2]]
+
+    def op(e, fn, reads, writes, acc=False):
+        rd, wr = [reg(x) for x in reads], [reg(x) for x in writes]
+        need(e, rd, wr, acc)
+        cnt[e] += 1
+        fn().then_inc(T.sem[SEM[e]], 1)
+        note(e, rd, wr, SEM[e], cnt[e])
+
+    def src(x):
+        if len(x) == 2:
+            return ap(x[0]).indirect(ap(x[1])), [x[0], x[1]]
+        return ap(x), [x]
+
+    def copy(out, a):
+        s, rd = src(a)
+        op("V", lambda: g.vector.tensor_copy(ap(out), s), rd, [out])
+
+    def tt(out, a, b, alu):
+        s, rd = src(a)
+        op("V", lambda: g.vector.tensor_tensor(ap(out), s, ap(b), alu), rd + [b], [out])
+
+    def ts(out, a, s1, o1, s2=None, o2=None):
+        s, rd = src(a)
+        v1 = ap(s1) if isinstance(s1, tuple) else s1
+        v2 = ap(s2) if isinstance(s2, tuple) else s2
+        rd = rd + [x for x in (s1, s2) if isinstance(x, tuple)]
+        if o2 is None:
+            op("V", lambda: g.vector.tensor_scalar(ap(out), s, v1, None, o1), rd, [out])
+        else:
+            op("V", lambda: g.vector.tensor_scalar(ap(out), s, v1, v2, o1, o2), rd, [out])
+
+    def red(out, a):
+        op("V", lambda: g.vector.tensor_reduce(ap(out), ap(a), AxisListType.X, ALU.add), [a], [out])
+
+    def fill(a, v):
+        op("V", lambda: g.vector.memset(ap(a), v), [], [a])
+
+    def scan(out, d0, d1, init, o0, o1):
+        iv = ap(init) if isinstance(init, tuple) else init
+        rd = [d0, d1] + ([init] if isinstance(init, tuple) else [])
+        op("V", lambda: g.vector.tensor_tensor_scan(ap(out), ap(d0), ap(d1), iv, o0, o1), rd, [out])
+
+    def act(out, a, func, bias=0.0, scale=1.0, accum=None):
+        s, rd = src(a)
+        bv = ap(bias) if isinstance(bias, tuple) else bias
+        rd = rd + ([bias] if isinstance(bias, tuple) else [])
+        if accum is None:
+            op("A", lambda: g.scalar.activation(ap(out), s, func, bias=bv, scale=scale), rd, [out])
+        else:
+            op("A", lambda: g.scalar.activation(ap(out), s, func, bias=bv, scale=scale, accum_out=ap(accum)), rd, [out, accum])
+
+    def mm(out, lhsT, rhs, start=True, stop=True):
+        op("P", lambda: g.tensor.matmul(ap(out), ap(lhsT), ap(rhs), start, stop), [lhsT, rhs], [out], acc=True)
+
+    def iota(out, pattern, base, cm):
+        if out[0] in ("pI", "W"):
+            op("G", lambda: g.iota(ap(out), pattern, base, cm), [], [out])
+        else:
+            op("G", lambda: g.iota(ap(out), pattern, base, cm, allow_small_or_imprecise_dtypes=True), [], [out])
+
+    def dma(e, pairs, sem, reads, writes):
+        need(e, reads, writes)
+        for o, i in pairs:
+            Q[e].dma_start(o, i).then_inc(T.sem[sem], 16)
+        note("D" + sem, reads, writes, sem, 16 * len(pairs))
+
+    every = [e for e in topo.engines(core, nxt) if all(e in topo.engines(core, c) for c in T.cores if c != core)]
+    engs = every[0::2]
+    mask = sum(1 << e for e in engs)
+    sent = [0]
+
+    def ship(buf, a, b, out, oa, ob, sem):
+        need("G", [(buf, a, b)], [])
+        rid, pid, _ = topo.addr(nxt)
+        g.remote_dma(out_ap=T[out][:, oa:ob], in_ap=T[buf][:, a:b], remote_sem=T.sem[sem], local_sem=T.sem.sent,
+                     pid=pid, routing_id=rid, dma_engine_mask=mask)
+        sent[0] += len(engs)
+        note("R", [], [(out, oa, ob)], sem, len(engs))
+
+    def share_aim(land, sem):
+        need("G", [(land, 4 * rank, 4 * rank + 1)], [])
+        others = [c for c in T.cores if c != core]
+        ids = [DstId(rid=topo.addr(c)[0], pnc=topo.addr(c)[1]) for c in others]
+        a = T[land][:, 4 * rank:4 * rank + 1]
+        g.remote_dma_fused([RemoteDMATransfer(dst_ids=ids, dma_engine_mask=mask, remote_sem=T.sem[sem], srcs=[a],
+                                              dsts=[a for c in others])], local_sem=T.sem.sent)
+        sent[0] += len(engs)
+        for k in range(N):
+            if k != rank:
+                note("R", [], [(land, 4 * k, 4 * k + 1)], sem, len(engs) * (N - 1))
+
+    dma("A", [(T.trI[:, 0:768], T.trait[:, 0:768])], "l_t0", [], [("trI", 0, 768)])
+    dma("S", [(T.mgI[:], T.mg[:])], "l_mg", [], [("mgI", 0, 32)])
+    dma("S", [(T.damI[:, 384:512], T.dam[:, 384:512])], "l_dam1", [], [("damI", 384, 512)])
+    dma("S", [(T.aimI[:], T.aim0[:])], "l_aim", [], [("aimI", 0, 1)])
+    dma("A", [(T.trI[:, 768:1536], T.trait[:, 768:1536])], "l_t1", [], [("trI", 768, 1536)])
+    dma("A", [(T.trI[:, 1536:2304], T.trait[:, 1536:2304])], "l_t2", [], [("trI", 1536, 2304)])
+    dma("A", [(T.trI[:, 2304:3072], T.trait[:, 2304:3072])], "l_t3", [], [("trI", 2304, 3072)])
+    dma("S", [(T.sireI[:, 0:192], T.sire[:, 0:192])], "l_sire", [("trI", 768, 1536)], [("sireI", 0, 192)])
+    dma("S", [(T.damI[:, 0:192], T.dam[:, 0:192])], "l_dam0", [], [("damI", 0, 192)])
+    iota(("pI", 0, 1), [[0, 1]], 0, 1)
+    iota(("Gm", 0, 128), [[16, 8], [0, 16]], 0, 0)
+    iota(("Y", 0, 143), [[1, 143]], 0, -1)
+    iota(("W", 1936, 3152), [[0, 1216]], 0, 0)
+    iota(("io", 0, 512), [[0, 32], [1, 16]], 0, 0)
+    fill(("W", 0, 1936), 0)
+    own = [4 * rank + k for k in range(4)]
+    d1, s2, d2 = [(4 * rank + 4 + k) % 16 for k in range(3)]
+    wp = [(T.W[own[0]:128:16, 0:3072], T.sire[:, 0:192])]
+    wp.append((T.W[d1:128:16, 0:3072], T.dam[:, 0:192]))
+    wp.append((T.W[s2:128:16, 0:3072], T.sire[:, 192:384]))
+    wp.append((T.W[d2:128:16, 0:3072], T.dam[:, 192:384]))
+    dma("S", wp, "l_w", [], [("W", 0, 3072)])
+    dma("S", [(T.sireI[:, 192:384], T.sire[:, 192:384])], "l_sire2", [], [("sireI", 192, 384)])
+    dma("S", [(T.damI[:, 192:384], T.dam[:, 192:384])], "l_dam2", [], [("damI", 192, 384)])
+
+    PM, PG, OWN, KB, PS1, PD1, PS2, PD2, Y0, Y1, T1 = [("cc", k, k + 1) for k in range(11)]
+    fill(("seg", 0, 1024), 1.0)
+    fill(("seg", 0, 1024, 16), 0.0)
+    ts(("pI", 1, 2), ("pI", 0, 1), 15, ALU.bitwise_and)
+    ts(("pI", 3, 4), ("pI", 0, 1), 16, ALU.bitwise_and, 4, ALU.logical_shift_right)
+    copy(PM, ("pI", 1, 2))
+    ts(("pI", 2, 3), ("pI", 1, 2), 2, ALU.logical_shift_right)
+    copy(Y1, ("pI", 3, 4))
+    tt(PG, ("pI", 0, 1), PM, ALU.subtract)
+    ts(OWN, ("pI", 2, 3), float(rank), ALU.is_equal)
+    for col, r in ((PS1, own[0]), (PD1, d1), (PS2, s2), (PD2, d2)):
+        ts(col, PM, float(r), ALU.is_equal)
+    ts(KB, PM, -1.0 / 64, ALU.mult, 15.0 / 64, ALU.add)
+    ts(Y0, Y1, -1.0, ALU.mult, 1.0, ALU.add)
+    ts(("blk", 0, 128), ("Gm", 0, 128), PG, ALU.is_equal)
+    for b, col in (("bs1", PS1), ("bd1", PD1), ("bs2", PS2), ("bd2", PD2)):
+        ts((b, 0, 128), ("blk", 0, 128), col, ALU.mult)
+    copy(("mg16", 0, 32), ("mgI", 0, 32))
+    ts(("damI", 512, 520), ("mgI", 16, 24), 6400.0, ALU.add)
+    ts(("damI", 520, 528), ("mgI", 8, 16), 6400.0, ALU.add)
+    A144 = (0, 144)
+    ts(("EI",) + A144, ("damI", 384, 528), -6400.0, ALU.add, 0.0, ALU.max)
+    ts(("AI",) + A144, ("EI",) + A144, 15, ALU.bitwise_and)
+    ts(("EF",) + A144, ("AI",) + A144, 3071.0, ALU.mult)
+    tt(("EG",) + A144, ("EF",) + A144, ("EI",) + A144, ALU.add)
+    ts(("pos16",) + A144, ("EG",) + A144, 0.0625, ALU.mult)
+    copy(T1, ("aimI", 0, 1))
+
+    def y_chunk(k):
+        a, b = 768 * k, 768 * k + 768
+        ts(("y1", a, b), ("trI", a, b), T1, ALU.subtract)
+
+    def f(n):
+        return (n, 0, 128)
+
+    y_chunk(0)
+    ts(("dmj", 0, 512), ("io", 0, 512), PM, ALU.is_equal)
+    ts(("dm", 0, 16), ("io", 0, 16), PM, ALU.is_equal)
+    ts(("ZS", 0, 143), ("Y", 0, 143), float(15 - s2), ALU.is_equal, PS2, ALU.mult)
+    ts(("ZD", 0, 143), ("Y", 0, 143), float(15 - d2), ALU.is_equal, PD2, ALU.mult)
+    ts(("dmo", 0, 16), ("dm", 0, 16), OWN, ALU.mult)
+    y_chunk(1)
+    ts(("dmh", 0, 16), ("dmo", 0, 16), 0.5, ALU.mult)
+    fill(("zero", 0, 512), 0.0)
+    fill(("tabA", 0, Z0), 0.0)
+    fill(("tabB", 0, Z0), 0.0)
+    y_chunk(2)
+    ts(("gs", 0, 128), (("trI", 0, 3072), ("mg16", 0, 8)), T1, ALU.subtract)
+    ship("gs", 0, 128, "y1", 3072, 3200, "a_g0")
+    y_chunk(3)
+    copy(("sire16", 0, 192), ("sireI", 0, 192))
+    copy(("dam16", 0, 192), ("damI", 0, 192))
+    ts(("ident", 0, 128), ("Y", 0, 128), 0.0, ALU.is_equal)
+    for y, m in ((0, Y0), (1, Y1)):
+        for h in range(2):
+            ts(("R%d%d" % (y, h), 0, 128), ("Y", 0, 128), 16.0 * (h - y), ALU.is_equal, m, ALU.mult)
+    dma("S", [(T.trI[r:128:16, 0:3072], T.sire[:, 192:384]) for r in own], "l_tr", [], [("trI", 0, 3072)])
+    for k in range(4):
+        act(("FH", 768 * k, 768 * k + 768), ("y1", 768 * k, 768 * k + 768), AF.Abs, 0.0, 0.5)
+
+    copy(("CF", 2048, 2304), (("W", 0, 3152), ("pos16", 128, 144)))
+    mm(("pC", 0, 128), ("bs1", 0, 128), ("CF", 2176, 2304))
+    mm(("pC", 128, 256), ("bd1", 0, 128), ("CF", 2176, 2304))
+    mm(("pC", 256, 384), ("bs2", 0, 128), ("CF", 2048, 2176))
+    mm(("pC", 384, 512), ("bd2", 0, 128), ("CF", 2048, 2176))
+    c = ("damI", 384, 512)
+    ts(f("q1"), c, 6272.0, ALU.is_lt)
+    ts(f("pp"), c, 6400.0, ALU.is_ge)
+    ts(f("qq"), c, 9472.0, ALU.is_ge)
+    ts(f("k1"), c, 6272.0, ALU.is_ge, 128.0, ALU.mult)
+    tt(f("is2"), f("pp"), f("qq"), ALU.subtract)
+    tt(f("xs"), f("q1"), c, ALU.mult)
+    tt(("mk", 0, 512), ("pC", 0, 512), ("dmj", 0, 512), ALU.mult)
+    tt(f("r1"), f("k1"), c, ALU.add)
+    scan(("msc", 0, 512), ("seg", 0, 512), ("mk", 0, 512), 0.0, ALU.mult, ALU.add)
+    ts(f("q3"), f("qq"), -3072.0, ALU.mult)
+    copy(("ms16", 0, 32), ("msc", 15, 512, 16))
+    MS1, MD1, MS2, MD2 = [("ms16", 8 * k, 8 * k + 8) for k in range(4)]
+    copy(("CF", 0, 1024), (("W", 0, 3152), ("pos16", 0, 64)))
+
+    def to_list(pb, z, flat, f0, o0):
+        for i in range(16):
+            mm((pb, o0, o0 + 64), (z, 15 - i, 143 - i), (flat, f0 + i, f0 + 1024, 16), i == 0, i == 15)
+
+    to_list("pS", "ZS", "CF", 0, 0)
+    to_list("pD", "ZD", "CF", 0, 0)
+
+    def u_lists(h):
+        v = lambda n: (n, 64 * h, 64 * h + 64)
+        tt(v("lS2"), v("is2"), v("pS"), ALU.mult)
+        tt(v("lD2"), v("is2"), v("pD"), ALU.mult)
+        tt(v("lS"), v("lS2"), v("PS"), ALU.add)
+        tt(v("lD"), v("lD2"), v("PD"), ALU.add)
+        copy(v("US16"), v("lS"))
+        copy(v("UD16"), v("lD"))
+
+    PART = [0]
+    for n in (512, 768, 896, 896):
+        PART.append(PART[-1] + n)
+
+    def sires1(k):
+        a, b = PART[k], PART[k + 1]
+        act(("tmp", a, b), (("FH", 0, 3072), ("sire16", a // 16, b // 16)), AF.Identity)
+
+    def dams1(tab, k):
+        a, b = PART[k], PART[k + 1]
+        tt((tab, Z0 + 3200 + a, Z0 + 3200 + b), (("FH", 0, 3200), ("dam16", a // 16, b // 16)), ("tmp", a, b), ALU.add)
+
+    def ghosts1_act(r):
+        act(("gt", 128 * r - 128, 128 * r), (("FH", 0, 3072), MS1), AF.Identity)
+
+    def ghosts1(r, tab):
+        o = 128 * r
+        tt(("gs", o, o + 128), (("FH", 0, 3200), MD1), ("gt", o - 128, o), ALU.add)
+        ship("gs", o, o + 128, tab, G1, G1 + 128, "a_g1%d" % r)
+
+    def ghosts2_act(r, tab):
+        act(("gt", 384 + 128 * (r - 1), 384 + 128 * r), ((tab, Z0, OWN1), MS2), AF.Identity)
+
+    def ghosts2(r, tab):
+        o = 384 + 128 * r
+        tt(("gs", o, o + 128), ((tab, Z0, G1X), MD2), ("gt", 384 + 128 * (r - 1), 384 + 128 * r), ALU.add)
+        ship("gs", o, o + 128, tab, G2X, G2X + 128, "a_g2%d" % r)
+
+    def double1(tab):
+        act((tab, G1X, G1X + 128), (tab, G1, G1 + 128), AF.Identity, 0.0, 2.0)
+
+    def double3(tab):
+        act((tab, X3, X3 + 1024), ("G3", 0, 1024), AF.Identity, 0.0, 0.5)
+
+    def ghosts3(r, tab):
+        o = 896 + 128 * (r - 2)
+        ts(("gs", o, o + 128), (("G3", 0, 1024), ("mg16", 24, 32)), 0.5, ALU.mult)
+        ship("gs", o, o + 128, tab, G3X, G3X + 128, "a_g3%d" % r)
+
+    tab = "tabA"
+    sires1(0)
+    sires1(1)
+    act(("FH", 3072, 3200), ("y1", 3072, 3200), AF.Abs, 0.0, 0.5)
+    ghosts1_act(1)
+    dams1(tab, 0)
+    ghosts1(1, tab)
+    dams1(tab, 1)
+    sires1(2)
+    sires1(3)
+    act((tab, Z0, Z0 + 3200), ("y1", 0, 3200), AF.Abs)
+    dams1(tab, 2)
+    dams1(tab, 3)
+    REST = [(CUT + 512 * k, CUT + 512 * k + 512, pb) for k, pb in enumerate(("pA", "pB", "pE"))]
+    copy(("sire16", 192, 384), ("sireI", 192, 384))
+    copy(("dam16", 192, 384), ("damI", 192, 384))
+    for n, (a, b, pb) in enumerate(REST):
+        if n == 1:
+            act(("tmp", 0, CUT), ((tab, Z0, OWN1), ("sire16", 192, 192 + CUT // 16)), AF.Identity)
+            ghosts2_act(1, tab)
+        act(("tmp", a, b), ((tab, Z0, OWN1), ("sire16", 192 + a // 16, 192 + b // 16)), AF.Identity)
+        mm((pb, 0, 512), ("ident", 0, 128), ("tmp", a, b), True, False)
+    double1(tab)
+    for a, b, pb in REST:
+        act(("tmp2", a - CUT, b - CUT), ((tab, Z0, G1X), ("dam16", 192 + a // 16, 192 + b // 16)), AF.Identity)
+        mm((pb, 0, 512), ("ident", 0, 128), ("tmp2", a - CUT, b - CUT), False, True)
+    copy(("CF", 1024, 2048), (("W", 0, 3152), ("pos16", 64, 128)))
+    dma("S", [(T.W[q:128:16, 0:3072], T.sire[:, 0:192]) for q in own[1:]], "l_w2", [], [("W", 0, 3072)])
+    tt(f("w8"), f("q1"), f("is2"), ALU.add)
+    ts(f("n2"), f("is2"), -1.0, ALU.mult, 1.0, ALU.add)
+    tt(f("r2"), f("r1"), f("q3"), ALU.add)
+    ts(f("lS"), f("w8"), float(Z0), ALU.mult)
+    tt(f("PD"), f("r2"), f("n2"), ALU.mult)
+    tt(f("PS"), f("xs"), f("lS"), ALU.add)
+    u_lists(0)
+    tt(("D2", 0, CUT), ((tab, Z0, G1X), ("dam16", 192, 192 + CUT // 16)), ("tmp", 0, CUT), ALU.add)
+    ghosts2(1, tab)
+    to_list("pS", "ZS", "CF", 1024, 64)
+    to_list("pD", "ZD", "CF", 1024, 64)
+    act(("T3", 0, 1024), ((tab, 0, OWN1), ("US16", 0, 64)), AF.Identity, KB)
+    JL, JB = [("cl", k, k + 1) for k in (0, 1)], [("cl", k, k + 1) for k in (2, 3)]
+    scan(("tmp", 0, CUT), ("D2", 0, CUT), ("D2", 0, CUT), 0.0, ALU.max, ALU.max)
+    scan(("FH", 0, CUT), ("D2", 0, CUT), ("D2", 0, CUT), 1.0e9, ALU.min, ALU.min)
+    for out, alu in (("tmp", ALU.max), ("FH", ALU.min)):
+        for a, b, pb in REST:
+            scan((out, a, b), (pb, 0, 512), ("zero", 0, 512), (out, a - 1, a), alu, ALU.add)
+    act(("junk", 0, 3072), ("tmp", 0, 3072), AF.Sign, ("tmp", 3071, 3072), -1.0, JL[0])
+    act(("junk", 0, 3072), ("FH", 0, 3072), AF.Sign, ("FH", 3071, 3072), -1.0, JB[0])
+
+    def chain(r, land):
+        b = lambda k: ("cl", 16 * r + k, 16 * r + k + 1)
+        ib = lambda k: ("ci", 16 * r + k, 16 * r + k + 1)
+        o = lambda k: ("sm16", 16 * r + 2 * k, 16 * r + 2 * k + 1)
+        lk = lambda k: ("lk", 64 * (r - 1) + 16 * k, 64 * (r - 1) + 16 * k + 16)
+        J = JL[r - 1]
+        if r == 2:
+            copy(o(0), J)
+            tt(lk(0), (("sf", 0, 1024), o(0)), ("dmo", 0, 16), ALU.mult)
+            red(b(0), lk(0))
+            J = b(0)
+        copy(ib(0), J)
+        ts(b(1), J, 0.0625, ALU.mult)
+        ts(ib(1), ib(0), 15, ALU.bitwise_and)
+        ts(o(1), ib(1), 191.9375, ALU.mult, b(1), ALU.add)
+        tt(lk(1), (("trI", 0, 3072), o(1)), ("dmo", 0, 16), ALU.mult)
+        red(b(2), lk(1))
+        s = b(2)
+        ts(ib(2), s, -3200.0, ALU.add, 0.0, ALU.max)
+        ts(b(3), s, 3200.0, ALU.is_lt, s, ALU.mult)
+        ts(ib(3), ib(2), 15, ALU.bitwise_and)
+        ts(b(4), ib(2), 0.0625, ALU.mult)
+        ts(b(5), s, 3200.0, ALU.is_ge)
+        ts(o(2), ib(3), 191.9375, ALU.mult, b(4), ALU.add)
+        tt(lk(2), (("W", 0, 3152), o(2)), ("dmo", 0, 16), ALU.mult)
+        red(b(6), lk(2))
+        ts(o(3), b(6), b(5), ALU.mult, b(3), ALU.add)
+        tt(lk(3), (("y1", 0, 3072), o(3)), ("dmh", 0, 16), ALU.mult)
+        red((land, 4 * rank, 4 * rank + 1), lk(3))
+
+    tt(("key", 0, 1024), ((tab, Z0, X3), ("UD16", 0, 64)), ("T3", 0, 1024), ALU.add)
+    chain(1, "land1")
+    share_aim("land1", "a_aim1")
+
+    def rows_a(between=None):
+        op("V", lambda: g.vector.transpose(T.D2[:, 1024:2048], T.key[:, 0:1024]), [("key", 0, 1024)], [("D2", 1024, 2048)])
+        if between:
+            between()
+        scan(("D2", 0, 1024), ("seg", 0, 1024), ("D2", 1024, 2048), 0.0, ALU.mult, ALU.max)
+
+    def rows_b():
+        ts(("ri", 0, 64), ("D2", 15, 1024, 16), 64.0, ALU.mult)
+        ts(("rb", 0, 64), ("ri", 0, 64), 15, ALU.bitwise_and)
+        copy(("rbf", 0, 64), ("rb", 0, 64))
+        for y in range(2):
+            for h in range(2):
+                mm(("pM", 32 * y, 32 * y + 32), ("R%d%d" % (y, h), 0, 128), ("rbf", h, 64, 2), h == 0, h == 1)
+
+    def rows_c(c0):
+        for y in range(2):
+            ts(("row16", c0 + y, c0 + 64, 2), ("pM", 32 * y, 32 * y + 32), -1.0, ALU.mult, 15.0, ALU.add)
+
+    def best_a(r):
+        k = 16 * (r - 1)
+        ts(("bR", k, k + 16), ("dm", 0, 16), JB[r - 1], ALU.mult, -1.0, ALU.mult)
+        mm(("pY", 128 + k, 144 + k), ("blk", 0, 128), ("bR", k, k + 16))
+
+    def best_b(r):
+        k = 16 * (r - 1)
+        copy(("bT", k, k + 16), ("pY", 128 + k, 144 + k))
+
+    def sire_cols(r):
+        act(("sf", 1024 * (r - 1), 1024 * r), (("bT", 16 * (r - 1), 16 * r), ("row16", 64 * (r - 1), 64 * r)), AF.Identity)
+        to_list("pY", "ZS", "sf", 1024 * (r - 1), 64 * (r - 1))
+
+    BH = [("cl", 4, 5), ("cl", 5, 6)]
+
+    def outputs(r, first):
+        ts(("yso", 64 * (r - 1), 64 * r), ("pY", 64 * (r - 1), 64 * r), float(first), ALU.add)
+        ts(("yto", r - 1, r), BH[r - 1], 2.0, ALU.mult, T1, ALU.add)
+
+    def aims(r, land):
+        op("V", lambda: g.vector.tensor_reduce(ap(BH[r - 1]), T[land][:, 0:16:4], AxisListType.X, ALU.add),
+           [(land, 0, 16)], [BH[r - 1]])
+
+    rows_a()
+    rows_b()
+    n = 48
+    best_a(1)
+    copy(("ci", n, n + 1), JB[0])
+    ts(("cl", n + 1, n + 2), JB[0], -0.0625, ALU.mult)
+    ts(("ci", n + 2, n + 3), ("ci", n, n + 1), -1.0, ALU.mult)
+    rows_c(0)
+    ts(("ci", n + 1, n + 2), ("ci", n + 2, n + 3), 15, ALU.bitwise_and)
+    ts(("sm16", n, n + 1), ("ci", n + 1, n + 2), 191.9375, ALU.mult, ("cl", n + 1, n + 2), ALU.add)
+    copy(("bg", 0, 16), (("W", 0, 3152), ("sm16", n, n + 1)))
+    mm(("pM", 256, 272), ("bs2", 0, 128), ("bg", 0, 16))
+    mm(("pM", 272, 288), ("bd2", 0, 128), ("bg", 0, 16))
+    aims(1, "land1")
+    best_b(1)
+    u_lists(1)
+    tt(("bm", 0, 32), ("pM", 256, 288), ("dmj", 0, 32), ALU.mult)
+    scan(("bsc", 0, 32), ("seg", 0, 32), ("bm", 0, 32), 0.0, ALU.mult, ALU.add)
+    copy(("sm16", n + 4, n + 8, 2), ("bsc", 15, 32, 16))
+    BS, BD = ("sm16", n + 4, n + 5), ("sm16", n + 6, n + 7)
+
+    def begin(r, tab):
+        bias = BH[r - 2]
+        for k in range(4):
+            act(("FH", 800 * k, 800 * k + 800), ("y1", 800 * k, 800 * k + 800), AF.Abs, bias, -0.5)
+        for k in range(3):
+            ts((tab, Z0 + 800 * k, Z0 + 800 * k + 800), ("FH", 800 * k, 800 * k + 800), 2.0, ALU.mult)
+        for k in range(4):
+            sires1(k)
+            dams1(tab, k)
+            if k == 0:
+                ghosts1_act(r)
+                ghosts1(r, tab)
+        act((tab, Z0 + 2400, Z0 + 3200), ("FH", 2400, 3200), AF.Identity, 0.0, 2.0)
+        ghosts2_act(r, tab)
+        copy(("ub1", 0, 16), ((tab, Z0, OWN1), BS))
+        tt(("Ub", 0, 16), ((tab, Z0, G1X), BD), ("ub1", 0, 16), ALU.add)
+        ghosts2(r, tab)
+        for k in range(2):
+            a, b = 512 * k, 512 * k + 512
+            act(("tmp2", a, b), (("Ub", 0, 16), ("row16", 32 * k, 32 * k + 32)), AF.Identity)
+            tt(("T3", a, b), ((tab, 0, OWN1), ("US16", 32 * k, 32 * k + 32)), ("tmp2", a, b), ALU.add)
+        double1(tab)
+        act(("T4", 0, 1024), ((tab, 0, OWN1), ("US16", 64, 128)), AF.Identity, KB if r == 2 else 0.0)
+        sire_cols(r - 1)
+        tt(("G3", 0, 1024), ((tab, Z0, X3), ("UD16", 0, 64)), ("T3", 0, 1024), ALU.add)
+
+    tab = "tabB"
+    begin(2, tab)
+    scan(("tmp", 0, 1024), ("G3", 0, 1024), ("G3", 0, 1024), 0.0, ALU.max, ALU.max)
+    act(("junk", 0, 1024), ("tmp", 0, 1024), AF.Sign, ("tmp", 1023, 1024), -1.0, JL[1])
+    double3(tab)
+    ghosts3(2, tab)
+    scan(("FH", 0, 1024), ("G3", 0, 1024), ("G3", 0, 1024), 1.0e9, ALU.min, ALU.min)
+    act(("junk", 0, 1024), ("FH", 0, 1024), AF.Sign, ("FH", 1023, 1024), -1.0, JB[1])
+    chain(2, "land2")
+    share_aim("land2", "a_aim2")
+    tt(("key", 0, 1024), ((tab, Z0, TW), ("UD16", 64, 128)), ("T4", 0, 1024), ALU.add)
+    rows_a(lambda: aims(2, "land2"))
+    rows_b()
+    best_a(2)
+    ts(("sm16", 58, 59), JB[1], -1.0, ALU.mult)
+    outputs(1, 6400)
+    rows_c(64)
+    best_b(2)
+
+    tab = "tabA"
+    begin(3, tab)
+    double3(tab)
+    ghosts3(3, tab)
+    ts(("HB", 0, 16), (("G3", 0, 1024), ("sm16", 58, 59)), 0.5, ALU.mult)
+    tt(("T3", 0, 1024), (("HB", 0, 16), ("row16", 64, 128)), ("T4", 0, 1024), ALU.add)
+    act(("yo", 0, 1024), ("G3", 0, 1024), AF.Identity, 65535.0, -0.25)
+    dma("S", [(T.yf[:, 0:1024], T.yo[:, 0:1024])], "o_f3", [("yo", 0, 1024)], [])
+    for k in range(2):
+        a, b = 512 * k, 512 * k + 512
+        tt(("key", a, b), ((tab, Z0, TW), ("UD16", 64 + 32 * k, 96 + 32 * k)), ("T3", a, b), ALU.add)
+        act(("yo", 1024 + a, 1024 + b), ("key", a, b), AF.Identity, 65535.0, -0.25)
+        dma("S", [(T.yf[:, 1024 + a:1024 + b], T.yo[:, 1024 + a:1024 + b])], "o_f4%s" % "ab"[k], [("yo", 1024 + a, 1024 + b)], [])
+        if k == 0:
+            outputs(2, 9600)
+            dma("S", [(T.ys[:], T.yso[:])], "o_ys", [("yso", 0, 128)], [])
+            dma("S", [(T.yt[:], T.yto[:])], "o_yt", [("yto", 0, 2)], [])
+
+    for s in sorted(total):
+        if known["G"].get(s, 0) < total[s]:
+            g.wait_ge(T.sem[s], total[s])
+    g.wait_ge(T.sem.sent, sent[0])

@@ -40,13 +40,14 @@ SCRATCH = {
     "gs": _sb(1152), "gt": _sb(768), "ri": _sb(64, I32), "rb": _sb(64, I32), "rbf": _sb(64, B16),
     "bT": _sb(32), "bR": _sb(32), "bg": _sb(16), "bm": _sb(32), "bsc": _sb(32), "Ub": _sb(16), "ub1": _sb(16), "HB": _sb(16),
     "cl": _sb(64), "ci": _sb(64, I32), "lk": _sb(128), "land1": _sb(16), "land2": _sb(16),
+    "off16": _sb(16, U16), "i16": _sb(16), "nm": _sb(256), "bg2": _sb(16), "bm2": _sb(16), "yt16": _sb(16),
     "yso": _sb(128), "yto": _sb(2),
 }
 BANKS = ("pC", "pS", "pD", "pM", "pY", "pA", "pB", "pE")
 for _b in BANKS:
     SCRATCH[_b] = ("psum", [128, 512], F32)
 SEMAPHORES = ["qV", "qA", "qP", "qG", "sent", "l_sire", "l_sire2", "l_dam0", "l_dam1", "l_dam2", "l_mg", "l_aim",
-              "l_t0", "l_t1", "l_t2", "l_t3", "l_w", "l_w2", "l_tr", "o_ys", "o_yt", "o_f3", "o_f4a", "o_f4b",
+              "l_t0", "l_t1", "l_t2", "l_t3", "l_w", "l_w2", "l_tr", "o_ys", "o_yt", "o_f3", "o_f4a", "o_f4b", "o_f4c",
               "a_g0", "a_g11", "a_g12", "a_g13", "a_g21", "a_g22", "a_g23", "a_g32", "a_g33", "a_aim1", "a_aim2"]
 
 
@@ -132,8 +133,8 @@ def rank_program(g, core, T, topo):
         else:
             op("V", lambda: g.vector.tensor_scalar(ap(out), s, v1, v2, o1, o2), rd, [out])
 
-    def red(out, a):
-        op("V", lambda: g.vector.tensor_reduce(ap(out), ap(a), AxisListType.X, ALU.add), [a], [out])
+    def red(out, a, alu=ALU.add):
+        op("V", lambda: g.vector.tensor_reduce(ap(out), ap(a), AxisListType.X, alu), [a], [out])
 
     def fill(a, v):
         op("V", lambda: g.vector.memset(ap(a), v), [], [a])
@@ -192,10 +193,10 @@ def rank_program(g, core, T, topo):
             if k != rank:
                 note("R", [], [(land, 4 * k, 4 * k + 1)], sem, len(engs) * (N - 1))
 
+    dma("A", [(T.damI[:, 384:512], T.dam[:, 384:512])], "l_dam1", [], [("damI", 384, 512)])
+    dma("S", [(T.aimI[:], T.aim0[:])], "l_aim", [], [("aimI", 0, 1)])
     dma("A", [(T.trI[:, 0:768], T.trait[:, 0:768])], "l_t0", [], [("trI", 0, 768)])
     dma("S", [(T.mgI[:], T.mg[:])], "l_mg", [], [("mgI", 0, 32)])
-    dma("S", [(T.damI[:, 384:512], T.dam[:, 384:512])], "l_dam1", [], [("damI", 384, 512)])
-    dma("S", [(T.aimI[:], T.aim0[:])], "l_aim", [], [("aimI", 0, 1)])
     dma("A", [(T.trI[:, 768:1536], T.trait[:, 768:1536])], "l_t1", [], [("trI", 768, 1536)])
     dma("A", [(T.trI[:, 1536:2304], T.trait[:, 1536:2304])], "l_t2", [], [("trI", 1536, 2304)])
     dma("A", [(T.trI[:, 2304:3072], T.trait[:, 2304:3072])], "l_t3", [], [("trI", 2304, 3072)])
@@ -204,9 +205,9 @@ def rank_program(g, core, T, topo):
     iota(("pI", 0, 1), [[0, 1]], 0, 1)
     iota(("Gm", 0, 128), [[16, 8], [0, 16]], 0, 0)
     iota(("Y", 0, 143), [[1, 143]], 0, -1)
-    iota(("W", 1936, 3152), [[0, 1216]], 0, 0)
     iota(("io", 0, 512), [[0, 32], [1, 16]], 0, 0)
-    fill(("W", 0, 1936), 0)
+    iota(("W", 800, 3152), [[0, 2352]], 0, 0)
+    fill(("W", 0, 800), 0)
     own = [4 * rank + k for k in range(4)]
     d1, s2, d2 = [(4 * rank + 4 + k) % 16 for k in range(3)]
     wp = [(T.W[own[0]:128:16, 0:3072], T.sire[:, 0:192])]
@@ -217,9 +218,9 @@ def rank_program(g, core, T, topo):
     dma("S", [(T.sireI[:, 192:384], T.sire[:, 192:384])], "l_sire2", [], [("sireI", 192, 384)])
     dma("S", [(T.damI[:, 192:384], T.dam[:, 192:384])], "l_dam2", [], [("damI", 192, 384)])
 
-    PM, PG, OWN, KB, PS1, PD1, PS2, PD2, Y0, Y1, T1 = [("cc", k, k + 1) for k in range(11)]
-    fill(("seg", 0, 1024), 1.0)
-    fill(("seg", 0, 1024, 16), 0.0)
+    PM, PG, OWN, KB, PS1, PD1, PS2, PD2, Y0, Y1, T1, HOWN = [("cc", k, k + 1) for k in range(12)]
+    fill(("seg", 0, 512), 1.0)
+    fill(("seg", 0, 512, 16), 0.0)
     ts(("pI", 1, 2), ("pI", 0, 1), 15, ALU.bitwise_and)
     ts(("pI", 3, 4), ("pI", 0, 1), 16, ALU.bitwise_and, 4, ALU.logical_shift_right)
     copy(PM, ("pI", 1, 2))
@@ -227,6 +228,7 @@ def rank_program(g, core, T, topo):
     copy(Y1, ("pI", 3, 4))
     tt(PG, ("pI", 0, 1), PM, ALU.subtract)
     ts(OWN, ("pI", 2, 3), float(rank), ALU.is_equal)
+    ts(HOWN, ("pI", 2, 3), float(rank), ALU.is_equal, 0.5, ALU.mult)
     for col, r in ((PS1, own[0]), (PD1, d1), (PS2, s2), (PD2, d2)):
         ts(col, PM, float(r), ALU.is_equal)
     ts(KB, PM, -1.0 / 64, ALU.mult, 15.0 / 64, ALU.add)
@@ -255,17 +257,22 @@ def rank_program(g, core, T, topo):
     y_chunk(0)
     ts(("dmj", 0, 512), ("io", 0, 512), PM, ALU.is_equal)
     ts(("dm", 0, 16), ("io", 0, 16), PM, ALU.is_equal)
+    ts(("i16", 0, 16), ("io", 0, 16), 0.0625, ALU.mult)
+    ts(("nm", 0, 256), ("dmj", 0, 256), -1.0e9, ALU.mult, 1.0e9, ALU.add)
     ts(("ZS", 0, 143), ("Y", 0, 143), float(15 - s2), ALU.is_equal, PS2, ALU.mult)
     ts(("ZD", 0, 143), ("Y", 0, 143), float(15 - d2), ALU.is_equal, PD2, ALU.mult)
     ts(("dmo", 0, 16), ("dm", 0, 16), OWN, ALU.mult)
     y_chunk(1)
     ts(("dmh", 0, 16), ("dmo", 0, 16), 0.5, ALU.mult)
-    fill(("zero", 0, 512), 0.0)
     fill(("tabA", 0, Z0), 0.0)
     fill(("tabB", 0, Z0), 0.0)
     y_chunk(2)
     ts(("gs", 0, 128), (("trI", 0, 3072), ("mg16", 0, 8)), T1, ALU.subtract)
     ship("gs", 0, 128, "y1", 3072, 3200, "a_g0")
+    half = ("seg", 512, 1024)
+    iota(half, [[0, 512]], 1, 0)
+    op("G", lambda: g.affine_select(ap(half), ap(half), [[0, 32], [1, 16]], ALU.not_equal, 0.0, 0, 0), [half], [half])
+    iota(("zero", 0, 512), [[0, 512]], 0, 0)
     y_chunk(3)
     copy(("sire16", 0, 192), ("sireI", 0, 192))
     copy(("dam16", 0, 192), ("damI", 0, 192))
@@ -277,11 +284,6 @@ def rank_program(g, core, T, topo):
     for k in range(4):
         act(("FH", 768 * k, 768 * k + 768), ("y1", 768 * k, 768 * k + 768), AF.Abs, 0.0, 0.5)
 
-    copy(("CF", 2048, 2304), (("W", 0, 3152), ("pos16", 128, 144)))
-    mm(("pC", 0, 128), ("bs1", 0, 128), ("CF", 2176, 2304))
-    mm(("pC", 128, 256), ("bd1", 0, 128), ("CF", 2176, 2304))
-    mm(("pC", 256, 384), ("bs2", 0, 128), ("CF", 2048, 2176))
-    mm(("pC", 384, 512), ("bd2", 0, 128), ("CF", 2048, 2176))
     c = ("damI", 384, 512)
     ts(f("q1"), c, 6272.0, ALU.is_lt)
     ts(f("pp"), c, 6400.0, ALU.is_ge)
@@ -289,13 +291,18 @@ def rank_program(g, core, T, topo):
     ts(f("k1"), c, 6272.0, ALU.is_ge, 128.0, ALU.mult)
     tt(f("is2"), f("pp"), f("qq"), ALU.subtract)
     tt(f("xs"), f("q1"), c, ALU.mult)
-    tt(("mk", 0, 512), ("pC", 0, 512), ("dmj", 0, 512), ALU.mult)
     tt(f("r1"), f("k1"), c, ALU.add)
-    scan(("msc", 0, 512), ("seg", 0, 512), ("mk", 0, 512), 0.0, ALU.mult, ALU.add)
     ts(f("q3"), f("qq"), -3072.0, ALU.mult)
+    copy(("CF", 2048, 2304), (("W", 0, 3152), ("pos16", 128, 144)))
+    mm(("pC", 0, 128), ("bs1", 0, 128), ("CF", 2176, 2304))
+    mm(("pC", 128, 256), ("bd1", 0, 128), ("CF", 2176, 2304))
+    mm(("pC", 256, 384), ("bs2", 0, 128), ("CF", 2048, 2176))
+    mm(("pC", 384, 512), ("bd2", 0, 128), ("CF", 2048, 2176))
+    copy(("CF", 0, 1024), (("W", 0, 3152), ("pos16", 0, 64)))
+    tt(("mk", 0, 512), ("pC", 0, 512), ("dmj", 0, 512), ALU.mult)
+    scan(("msc", 0, 512), ("seg", 0, 512), ("mk", 0, 512), 0.0, ALU.mult, ALU.add)
     copy(("ms16", 0, 32), ("msc", 15, 512, 16))
     MS1, MD1, MS2, MD2 = [("ms16", 8 * k, 8 * k + 8) for k in range(4)]
-    copy(("CF", 0, 1024), (("W", 0, 3152), ("pos16", 0, 64)))
 
     def to_list(pb, z, flat, f0, o0):
         for i in range(16):
@@ -355,12 +362,12 @@ def rank_program(g, core, T, topo):
     tab = "tabA"
     sires1(0)
     sires1(1)
+    sires1(2)
     act(("FH", 3072, 3200), ("y1", 3072, 3200), AF.Abs, 0.0, 0.5)
-    ghosts1_act(1)
     dams1(tab, 0)
+    ghosts1_act(1)
     ghosts1(1, tab)
     dams1(tab, 1)
-    sires1(2)
     sires1(3)
     act((tab, Z0, Z0 + 3200), ("y1", 0, 3200), AF.Abs)
     dams1(tab, 2)
@@ -378,14 +385,14 @@ def rank_program(g, core, T, topo):
     for a, b, pb in REST:
         act(("tmp2", a - CUT, b - CUT), ((tab, Z0, G1X), ("dam16", 192 + a // 16, 192 + b // 16)), AF.Identity)
         mm((pb, 0, 512), ("ident", 0, 128), ("tmp2", a - CUT, b - CUT), False, True)
-    copy(("CF", 1024, 2048), (("W", 0, 3152), ("pos16", 64, 128)))
-    dma("S", [(T.W[q:128:16, 0:3072], T.sire[:, 0:192]) for q in own[1:]], "l_w2", [], [("W", 0, 3072)])
     tt(f("w8"), f("q1"), f("is2"), ALU.add)
     ts(f("n2"), f("is2"), -1.0, ALU.mult, 1.0, ALU.add)
     tt(f("r2"), f("r1"), f("q3"), ALU.add)
     ts(f("lS"), f("w8"), float(Z0), ALU.mult)
     tt(f("PD"), f("r2"), f("n2"), ALU.mult)
     tt(f("PS"), f("xs"), f("lS"), ALU.add)
+    copy(("CF", 1024, 2048), (("W", 0, 3152), ("pos16", 64, 128)))
+    dma("S", [(T.W[q:128:16, 0:3072], T.sire[:, 0:192]) for q in own[1:]], "l_w2", [], [("W", 0, 3072)])
     u_lists(0)
     tt(("D2", 0, CUT), ((tab, Z0, G1X), ("dam16", 192, 192 + CUT // 16)), ("tmp", 0, CUT), ALU.add)
     ghosts2(1, tab)
@@ -395,50 +402,71 @@ def rank_program(g, core, T, topo):
     JL, JB = [("cl", k, k + 1) for k in (0, 1)], [("cl", k, k + 1) for k in (2, 3)]
     scan(("tmp", 0, CUT), ("D2", 0, CUT), ("D2", 0, CUT), 0.0, ALU.max, ALU.max)
     scan(("FH", 0, CUT), ("D2", 0, CUT), ("D2", 0, CUT), 1.0e9, ALU.min, ALU.min)
+    K, K2, LAST = ("cl", 8, 9), ("cl", 9, 10), ("tmp", 3071, 3072)
     for out, alu in (("tmp", ALU.max), ("FH", ALU.min)):
-        for a, b, pb in REST:
+        for n, (a, b, pb) in enumerate(REST):
             scan((out, a, b), (pb, 0, 512), ("zero", 0, 512), (out, a - 1, a), alu, ALU.add)
-    act(("junk", 0, 3072), ("tmp", 0, 3072), AF.Sign, ("tmp", 3071, 3072), -1.0, JL[0])
+            if out == "FH" and n == 0:
+                act(("junk", 0, 192), ("tmp", 15, 3072, 16), AF.Sign, LAST, -1.0, K)
+                ts(("off16", 0, 16), ("i16", 0, 16), K, ALU.add, 16.0, ALU.mult)
+                tt(("mk", 0, 256), (("tmp", 0, 3072), ("off16", 0, 16)), ("nm", 0, 256), ALU.max)
+                act(("junk", 0, 256), ("mk", 0, 256), AF.Sign, LAST, -1.0, K2)
+    ts(JL[0], K, 16.0, ALU.mult, K2, ALU.add)
     act(("junk", 0, 3072), ("FH", 0, 3072), AF.Sign, ("FH", 3071, 3072), -1.0, JB[0])
 
-    def chain(r, land):
-        b = lambda k: ("cl", 16 * r + k, 16 * r + k + 1)
-        ib = lambda k: ("ci", 16 * r + k, 16 * r + k + 1)
-        o = lambda k: ("sm16", 16 * r + 2 * k, 16 * r + 2 * k + 1)
-        lk = lambda k: ("lk", 64 * (r - 1) + 16 * k, 64 * (r - 1) + 16 * k + 16)
-        J = JL[r - 1]
-        if r == 2:
-            copy(o(0), J)
-            tt(lk(0), (("sf", 0, 1024), o(0)), ("dmo", 0, 16), ALU.mult)
-            red(b(0), lk(0))
-            J = b(0)
-        copy(ib(0), J)
-        ts(b(1), J, 0.0625, ALU.mult)
+    def founder_a(s, n):
+        b = lambda k: ("cl", n + k, n + k + 1)
+        ib = lambda k: ("ci", n + k, n + k + 1)
+        ts(ib(0), s, -3200.0, ALU.add, 0.0, ALU.max)
+        ts(b(0), s, 3200.0, ALU.is_lt, s, ALU.mult)
         ts(ib(1), ib(0), 15, ALU.bitwise_and)
-        ts(o(1), ib(1), 191.9375, ALU.mult, b(1), ALU.add)
-        tt(lk(1), (("trI", 0, 3072), o(1)), ("dmo", 0, 16), ALU.mult)
-        red(b(2), lk(1))
-        s = b(2)
-        ts(ib(2), s, -3200.0, ALU.add, 0.0, ALU.max)
-        ts(b(3), s, 3200.0, ALU.is_lt, s, ALU.mult)
-        ts(ib(3), ib(2), 15, ALU.bitwise_and)
-        ts(b(4), ib(2), 0.0625, ALU.mult)
-        ts(b(5), s, 3200.0, ALU.is_ge)
-        ts(o(2), ib(3), 191.9375, ALU.mult, b(4), ALU.add)
-        tt(lk(2), (("W", 0, 3152), o(2)), ("dmo", 0, 16), ALU.mult)
-        red(b(6), lk(2))
-        ts(o(3), b(6), b(5), ALU.mult, b(3), ALU.add)
-        tt(lk(3), (("y1", 0, 3072), o(3)), ("dmh", 0, 16), ALU.mult)
-        red((land, 4 * rank, 4 * rank + 1), lk(3))
+        ts(b(1), ib(0), 0.0625, ALU.mult)
+        ts(b(2), s, 3200.0, ALU.is_ge)
+        ts(("sm16", n, n + 1), ib(1), 191.9375, ALU.mult, b(1), ALU.add)
+        return ("sm16", n, n + 1)
 
-    tt(("key", 0, 1024), ((tab, Z0, X3), ("UD16", 0, 64)), ("T3", 0, 1024), ALU.add)
-    chain(1, "land1")
+    def founder_b(n):
+        ts(("sm16", n + 2, n + 3), ("cl", n + 3, n + 4), ("cl", n + 2, n + 3), ALU.mult, ("cl", n, n + 1), ALU.add)
+        return ("sm16", n + 2, n + 3)
+
+    def chain1(land):
+        J = JL[0]
+        ts(("ci", 16, 17), J, 240.0, ALU.add)
+        ts(("cl", 16, 17), J, 0.0625, ALU.mult, 15.0, ALU.add)
+        ts(("ci", 17, 18), ("ci", 16, 17), 15, ALU.bitwise_and)
+        ts(("sm16", 16, 17), ("ci", 17, 18), 191.9375, ALU.mult, ("cl", 16, 17), ALU.add)
+        tt(("lk", 0, 16), (("trI", 0, 3072), ("sm16", 16, 17)), ("dmo", 0, 16), ALU.mult)
+        red(("cl", 17, 18), ("lk", 0, 16))
+        tt(("lk", 16, 32), (("W", 0, 3152), founder_a(("cl", 17, 18), 20)), ("dmo", 0, 16), ALU.mult)
+        red(("cl", 23, 24), ("lk", 16, 32))
+        tt(("lk", 32, 48), (("y1", 0, 3072), founder_b(20)), ("dmh", 0, 16), ALU.mult)
+        red((land, 4 * rank, 4 * rank + 1), ("lk", 32, 48))
+
+    def best_lines_a():
+        copy(("bg2", 0, 16), (("W", 0, 3152), founder_a(("bsc", 15, 16), 32)))
+        mm(("pM", 288, 304), ("bs1", 0, 128), ("bg2", 0, 16))
+
+    def best_lines_b():
+        tt(("bm2", 0, 16), ("pM", 288, 304), ("dm", 0, 16), ALU.mult)
+        red(("cl", 35, 36), ("bm2", 0, 16))
+        ts(("yt16", 0, 16), (("y1", 0, 3072), founder_b(32)), 65536.0, ALU.add)
+
+    def chain2(land):
+        copy(("sm16", 40, 41), JL[1])
+        tt(("lk", 48, 64), (("sf", 0, 1024), ("sm16", 40, 41)), ("dm", 0, 16), ALU.mult)
+        red(("cl", 40, 41), ("lk", 48, 64))
+        ts(("lk", 64, 80), ("bT", 0, 16), ("cl", 40, 41), ALU.is_equal)
+        tt(("lk", 80, 96), ("lk", 64, 80), ("yt16", 0, 16), ALU.mult)
+        red(("cl", 41, 42), ("lk", 80, 96), ALU.max)
+        ts((land, 4 * rank, 4 * rank + 1), ("cl", 41, 42), -65536.0, ALU.add, HOWN, ALU.mult)
+
+    chain1("land1")
     share_aim("land1", "a_aim1")
+    tt(("key", 0, 1024), ((tab, Z0, X3), ("UD16", 0, 64)), ("T3", 0, 1024), ALU.add)
 
-    def rows_a(between=None):
+    def rows_a(between):
         op("V", lambda: g.vector.transpose(T.D2[:, 1024:2048], T.key[:, 0:1024]), [("key", 0, 1024)], [("D2", 1024, 2048)])
-        if between:
-            between()
+        between()
         scan(("D2", 0, 1024), ("seg", 0, 1024), ("D2", 1024, 2048), 0.0, ALU.mult, ALU.max)
 
     def rows_b():
@@ -476,7 +504,7 @@ def rank_program(g, core, T, topo):
         op("V", lambda: g.vector.tensor_reduce(ap(BH[r - 1]), T[land][:, 0:16:4], AxisListType.X, ALU.add),
            [(land, 0, 16)], [BH[r - 1]])
 
-    rows_a()
+    rows_a(lambda: aims(1, "land1"))
     rows_b()
     n = 48
     best_a(1)
@@ -489,9 +517,7 @@ def rank_program(g, core, T, topo):
     copy(("bg", 0, 16), (("W", 0, 3152), ("sm16", n, n + 1)))
     mm(("pM", 256, 272), ("bs2", 0, 128), ("bg", 0, 16))
     mm(("pM", 272, 288), ("bd2", 0, 128), ("bg", 0, 16))
-    aims(1, "land1")
     best_b(1)
-    u_lists(1)
     tt(("bm", 0, 32), ("pM", 256, 288), ("dmj", 0, 32), ALU.mult)
     scan(("bsc", 0, 32), ("seg", 0, 32), ("bm", 0, 32), 0.0, ALU.mult, ALU.add)
     copy(("sm16", n + 4, n + 8, 2), ("bsc", 15, 32, 16))
@@ -501,7 +527,8 @@ def rank_program(g, core, T, topo):
         bias = BH[r - 2]
         for k in range(4):
             act(("FH", 800 * k, 800 * k + 800), ("y1", 800 * k, 800 * k + 800), AF.Abs, bias, -0.5)
-        for k in range(3):
+        nv = 2 if r == 2 else 3
+        for k in range(nv):
             ts((tab, Z0 + 800 * k, Z0 + 800 * k + 800), ("FH", 800 * k, 800 * k + 800), 2.0, ALU.mult)
         for k in range(4):
             sires1(k)
@@ -509,18 +536,26 @@ def rank_program(g, core, T, topo):
             if k == 0:
                 ghosts1_act(r)
                 ghosts1(r, tab)
-        act((tab, Z0 + 2400, Z0 + 3200), ("FH", 2400, 3200), AF.Identity, 0.0, 2.0)
+                if r == 2:
+                    best_lines_a()
+        act((tab, Z0 + 800 * nv, Z0 + 3200), ("FH", 800 * nv, 3200), AF.Identity, 0.0, 2.0)
         ghosts2_act(r, tab)
         copy(("ub1", 0, 16), ((tab, Z0, OWN1), BS))
         tt(("Ub", 0, 16), ((tab, Z0, G1X), BD), ("ub1", 0, 16), ALU.add)
         ghosts2(r, tab)
+        if r == 2:
+            best_lines_b()
         for k in range(2):
             a, b = 512 * k, 512 * k + 512
             act(("tmp2", a, b), (("Ub", 0, 16), ("row16", 32 * k, 32 * k + 32)), AF.Identity)
             tt(("T3", a, b), ((tab, 0, OWN1), ("US16", 32 * k, 32 * k + 32)), ("tmp2", a, b), ALU.add)
         double1(tab)
+        if r == 2:
+            u_lists(1)
+            sire_cols(1)
         act(("T4", 0, 1024), ((tab, 0, OWN1), ("US16", 64, 128)), AF.Identity, KB if r == 2 else 0.0)
-        sire_cols(r - 1)
+        if r == 3:
+            sire_cols(2)
         tt(("G3", 0, 1024), ((tab, Z0, X3), ("UD16", 0, 64)), ("T3", 0, 1024), ALU.add)
 
     tab = "tabB"
@@ -531,7 +566,7 @@ def rank_program(g, core, T, topo):
     ghosts3(2, tab)
     scan(("FH", 0, 1024), ("G3", 0, 1024), ("G3", 0, 1024), 1.0e9, ALU.min, ALU.min)
     act(("junk", 0, 1024), ("FH", 0, 1024), AF.Sign, ("FH", 1023, 1024), -1.0, JB[1])
-    chain(2, "land2")
+    chain2("land2")
     share_aim("land2", "a_aim2")
     tt(("key", 0, 1024), ((tab, Z0, TW), ("UD16", 64, 128)), ("T4", 0, 1024), ALU.add)
     rows_a(lambda: aims(2, "land2"))
@@ -550,11 +585,12 @@ def rank_program(g, core, T, topo):
     tt(("T3", 0, 1024), (("HB", 0, 16), ("row16", 64, 128)), ("T4", 0, 1024), ALU.add)
     act(("yo", 0, 1024), ("G3", 0, 1024), AF.Identity, 65535.0, -0.25)
     dma("S", [(T.yf[:, 0:1024], T.yo[:, 0:1024])], "o_f3", [("yo", 0, 1024)], [])
-    for k in range(2):
-        a, b = 512 * k, 512 * k + 512
-        tt(("key", a, b), ((tab, Z0, TW), ("UD16", 64 + 32 * k, 96 + 32 * k)), ("T3", a, b), ALU.add)
+    b = 0
+    for k, n in enumerate((384, 384, 256)):
+        a, b = b, b + n
+        tt(("key", a, b), ((tab, Z0, TW), ("UD16", 64 + a // 16, 64 + b // 16)), ("T3", a, b), ALU.add)
         act(("yo", 1024 + a, 1024 + b), ("key", a, b), AF.Identity, 65535.0, -0.25)
-        dma("S", [(T.yf[:, 1024 + a:1024 + b], T.yo[:, 1024 + a:1024 + b])], "o_f4%s" % "ab"[k], [("yo", 1024 + a, 1024 + b)], [])
+        dma("S", [(T.yf[:, 1024 + a:1024 + b], T.yo[:, 1024 + a:1024 + b])], "o_f4%s" % "abc"[k], [("yo", 1024 + a, 1024 + b)], [])
         if k == 0:
             outputs(2, 9600)
             dma("S", [(T.ys[:], T.yso[:])], "o_ys", [("yso", 0, 128)], [])

@@ -7,12 +7,15 @@ F32, I32, U16, B16 = "float32", "int32", "uint16", "bfloat16"
 Z0 = 8
 OWN1 = Z0 + 6272
 G1 = Z0 + 6272
-G1X = Z0 + 6400
-G2X = Z0 + 6528
-X3 = Z0 + 6656
-G3X = Z0 + 7680
-TW = Z0 + 7808
-CUT = 1536
+E1 = Z0 + 6400
+G2X = Z0 + 6400
+X3 = Z0 + 6528
+G3X = Z0 + 7552
+TW = Z0 + 7680
+WW = 3080
+KP = 512
+VD = 1024
+CUT = 2048
 
 
 def _sb(n, d=F32):
@@ -21,28 +24,28 @@ def _sb(n, d=F32):
 
 SCRATCH = {
     "sireI": _sb(384, I32), "damI": _sb(528, I32), "mgI": _sb(32, I32), "aimI": _sb(1, I32),
-    "trI": _sb(3072, I32), "W": _sb(3152, I32),
+    "trI": _sb(3072, I32), "W": _sb(WW, I32),
     "y1": _sb(3200), "FH": _sb(3200), "tabA": _sb(TW), "tabB": _sb(TW),
-    "tmp": _sb(3072), "tmp2": _sb(1536), "D2": _sb(2048), "CF": _sb(2304),
+    "tmp": _sb(3072), "tmp2": _sb(1024), "D2": _sb(2048), "DT": _sb(1024), "KS": _sb(1024), "CF": _sb(2304),
     "T3": _sb(1024), "T4": _sb(1024), "key": _sb(1024), "G3": _sb(1024),
-    "yo": _sb(2048), "sf": _sb(2048), "seg": _sb(1024), "zero": _sb(512),
+    "yo": _sb(2048), "sf": _sb(2048), "sy": _sb(1024), "seg": _sb(1024), "zero": _sb(512),
     "io": _sb(512), "dmj": _sb(512), "mk": _sb(512), "msc": _sb(512), "junk": _sb(3072, B16),
     "Y": _sb(143), "Gm": _sb(128), "blk": _sb(128), "bs1": _sb(128), "bd1": _sb(128), "bs2": _sb(128), "bd2": _sb(128),
-    "ident": _sb(128), "ZS": _sb(143), "ZD": _sb(143),
+    "ident": _sb(128), "idm": _sb(128), "id8": _sb(128), "ZS": _sb(143), "ZD": _sb(143),
+    "w1": _sb(512), "w2": _sb(144), "w3": _sb(128),
     "R00": _sb(128, B16), "R01": _sb(128, B16), "R10": _sb(128, B16), "R11": _sb(128, B16),
-    "pI": _sb(8, I32), "cc": _sb(32), "dm": _sb(16), "dmo": _sb(16), "dmh": _sb(16),
+    "pI": _sb(8, I32), "cc": _sb(32), "dmo": _sb(16), "dmh": _sb(16),
     "sire16": _sb(384, U16), "dam16": _sb(384, U16), "mg16": _sb(32, U16), "ms16": _sb(32, U16),
     "pos16": _sb(144, U16), "US16": _sb(128, U16), "UD16": _sb(128, U16), "row16": _sb(128, U16), "sm16": _sb(64, U16),
-    "EI": _sb(144, I32), "AI": _sb(144, I32), "EF": _sb(144), "EG": _sb(144),
-    "q1": _sb(128), "pp": _sb(128), "qq": _sb(128), "is2": _sb(128), "xs": _sb(128), "w8": _sb(128), "PS": _sb(128),
-    "k1": _sb(128), "q3": _sb(128), "r1": _sb(128), "r2": _sb(128), "n2": _sb(128), "PD": _sb(128),
-    "lS": _sb(128), "lD": _sb(128), "lS2": _sb(128), "lD2": _sb(128),
+    "EI": _sb(144, I32), "AI": _sb(144, I32), "EF": _sb(144), "EG": _sb(144), "EM": _sb(144),
+    "pp": _sb(144), "qq": _sb(144), "is2": _sb(144), "mn": _sb(128), "x1": _sb(128),
     "gs": _sb(1152), "gt": _sb(768), "ri": _sb(64, I32), "rb": _sb(64, I32), "rbf": _sb(64, B16),
     "bT": _sb(32), "bR": _sb(32), "bg": _sb(16), "bm": _sb(32), "bsc": _sb(32), "Ub": _sb(16), "ub1": _sb(16), "HB": _sb(16),
     "cl": _sb(64), "ci": _sb(64, I32), "lk": _sb(128), "land1": _sb(16), "land2": _sb(16),
     "off16": _sb(16, U16), "i16": _sb(16), "nm": _sb(256), "bg2": _sb(16), "bm2": _sb(16), "yt16": _sb(16),
     "yso": _sb(128), "yto": _sb(2),
 }
+del SCRATCH["DT"], SCRATCH["KS"]
 BANKS = ("pC", "pS", "pD", "pM", "pY", "pA", "pB", "pE")
 for _b in BANKS:
     SCRATCH[_b] = ("psum", [128, 512], F32)
@@ -139,6 +142,9 @@ def rank_program(g, core, T, topo):
     def fill(a, v):
         op("V", lambda: g.vector.memset(ap(a), v), [], [a])
 
+    def turn(out, a):
+        op("V", lambda: g.vector.transpose(ap(out), ap(a)), [a], [out])
+
     def scan(out, d0, d1, init, o0, o1):
         iv = ap(init) if isinstance(init, tuple) else init
         rd = [d0, d1] + ([init] if isinstance(init, tuple) else [])
@@ -147,11 +153,12 @@ def rank_program(g, core, T, topo):
     def act(out, a, func, bias=0.0, scale=1.0, accum=None):
         s, rd = src(a)
         bv = ap(bias) if isinstance(bias, tuple) else bias
-        rd = rd + ([bias] if isinstance(bias, tuple) else [])
+        sv = ap(scale) if isinstance(scale, tuple) else scale
+        rd = rd + [x for x in (bias, scale) if isinstance(x, tuple)]
         if accum is None:
-            op("A", lambda: g.scalar.activation(ap(out), s, func, bias=bv, scale=scale), rd, [out])
+            op("A", lambda: g.scalar.activation(ap(out), s, func, bias=bv, scale=sv), rd, [out])
         else:
-            op("A", lambda: g.scalar.activation(ap(out), s, func, bias=bv, scale=scale, accum_out=ap(accum)), rd, [out, accum])
+            op("A", lambda: g.scalar.activation(ap(out), s, func, bias=bv, scale=sv, accum_out=ap(accum)), rd, [out, accum])
 
     def mm(out, lhsT, rhs, start=True, stop=True):
         op("P", lambda: g.tensor.matmul(ap(out), ap(lhsT), ap(rhs), start, stop), [lhsT, rhs], [out], acc=True)
@@ -168,8 +175,7 @@ def rank_program(g, core, T, topo):
             Q[e].dma_start(o, i).then_inc(T.sem[sem], 16)
         note("D" + sem, reads, writes, sem, 16 * len(pairs))
 
-    every = [e for e in topo.engines(core, nxt) if all(e in topo.engines(core, c) for c in T.cores if c != core)]
-    engs = every[0::2]
+    engs = [e for e in topo.engines(core, nxt) if all(e in topo.engines(core, c) for c in T.cores if c != core)]
     mask = sum(1 << e for e in engs)
     sent = [0]
 
@@ -194,9 +200,9 @@ def rank_program(g, core, T, topo):
                 note("R", [], [(land, 4 * k, 4 * k + 1)], sem, len(engs) * (N - 1))
 
     dma("A", [(T.damI[:, 384:512], T.dam[:, 384:512])], "l_dam1", [], [("damI", 384, 512)])
+    dma("S", [(T.mgI[:], T.mg[:])], "l_mg", [], [("mgI", 0, 32)])
     dma("S", [(T.aimI[:], T.aim0[:])], "l_aim", [], [("aimI", 0, 1)])
     dma("A", [(T.trI[:, 0:768], T.trait[:, 0:768])], "l_t0", [], [("trI", 0, 768)])
-    dma("S", [(T.mgI[:], T.mg[:])], "l_mg", [], [("mgI", 0, 32)])
     dma("A", [(T.trI[:, 768:1536], T.trait[:, 768:1536])], "l_t1", [], [("trI", 768, 1536)])
     dma("A", [(T.trI[:, 1536:2304], T.trait[:, 1536:2304])], "l_t2", [], [("trI", 1536, 2304)])
     dma("A", [(T.trI[:, 2304:3072], T.trait[:, 2304:3072])], "l_t3", [], [("trI", 2304, 3072)])
@@ -206,21 +212,22 @@ def rank_program(g, core, T, topo):
     iota(("Gm", 0, 128), [[16, 8], [0, 16]], 0, 0)
     iota(("Y", 0, 143), [[1, 143]], 0, -1)
     iota(("io", 0, 512), [[0, 32], [1, 16]], 0, 0)
-    iota(("W", 800, 3152), [[0, 2352]], 0, 0)
+    iota(("W", 800, WW), [[0, WW - 800]], 0, 0)
+    iota(("zero", 0, 512), [[0, 512]], 0, 0)
+    iota(("tabA", 0, Z0), [[0, Z0]], 0, 0)
+    iota(("tabB", 0, Z0), [[0, Z0]], 0, 0)
     fill(("W", 0, 800), 0)
     own = [4 * rank + k for k in range(4)]
     d1, s2, d2 = [(4 * rank + 4 + k) % 16 for k in range(3)]
-    wp = [(T.W[own[0]:128:16, 0:3072], T.sire[:, 0:192])]
-    wp.append((T.W[d1:128:16, 0:3072], T.dam[:, 0:192]))
-    wp.append((T.W[s2:128:16, 0:3072], T.sire[:, 192:384]))
-    wp.append((T.W[d2:128:16, 0:3072], T.dam[:, 192:384]))
-    dma("S", wp, "l_w", [], [("W", 0, 3072)])
+    wp = [(T.W[own[0]:128:16, 8:WW], T.sire[:, 0:192])]
+    wp.append((T.W[d1:128:16, 8:WW], T.dam[:, 0:192]))
+    wp.append((T.W[s2:128:16, 8:WW], T.sire[:, 192:384]))
+    wp.append((T.W[d2:128:16, 8:WW], T.dam[:, 192:384]))
+    dma("S", wp, "l_w", [], [("W", 8, WW)])
     dma("S", [(T.sireI[:, 192:384], T.sire[:, 192:384])], "l_sire2", [], [("sireI", 192, 384)])
     dma("S", [(T.damI[:, 192:384], T.dam[:, 192:384])], "l_dam2", [], [("damI", 192, 384)])
 
-    PM, PG, OWN, KB, PS1, PD1, PS2, PD2, Y0, Y1, T1, HOWN = [("cc", k, k + 1) for k in range(12)]
-    fill(("seg", 0, 512), 1.0)
-    fill(("seg", 0, 512, 16), 0.0)
+    PM, PG, OWN, KB, PS1, PD1, PS2, PD2, Y0, Y1, T1, HOWN, NS2, ND2, NY0, NY1 = [("cc", k, k + 1) for k in range(16)]
     ts(("pI", 1, 2), ("pI", 0, 1), 15, ALU.bitwise_and)
     ts(("pI", 3, 4), ("pI", 0, 1), 16, ALU.bitwise_and, 4, ALU.logical_shift_right)
     copy(PM, ("pI", 1, 2))
@@ -231,20 +238,39 @@ def rank_program(g, core, T, topo):
     ts(HOWN, ("pI", 2, 3), float(rank), ALU.is_equal, 0.5, ALU.mult)
     for col, r in ((PS1, own[0]), (PD1, d1), (PS2, s2), (PD2, d2)):
         ts(col, PM, float(r), ALU.is_equal)
+    for col, r in ((NS2, s2), (ND2, d2)):
+        ts(col, PM, float(r), ALU.is_equal, -1.0, ALU.mult)
     ts(KB, PM, -1.0 / 64, ALU.mult, 15.0 / 64, ALU.add)
     ts(Y0, Y1, -1.0, ALU.mult, 1.0, ALU.add)
-    ts(("blk", 0, 128), ("Gm", 0, 128), PG, ALU.is_equal)
+    ts(NY1, Y1, -1.0, ALU.mult)
+    ts(NY0, Y1, -1.0, ALU.add)
+    act(("w3", 0, 128), ("Gm", 0, 128), AF.Abs, PG, -1.0)
+    act(("blk", 0, 128), ("w3", 0, 128), AF.Relu, 1.0, -1.0)
     for b, col in (("bs1", PS1), ("bd1", PD1), ("bs2", PS2), ("bd2", PD2)):
-        ts((b, 0, 128), ("blk", 0, 128), col, ALU.mult)
+        act((b, 0, 128), ("blk", 0, 128), AF.Identity, 0.0, col)
+    for zb, k, m, nm in (("ZS", 15 - s2, PS2, NS2), ("ZD", 15 - d2, PD2, ND2)):
+        act(("w2", 0, 143), ("Y", 0, 143), AF.Abs, float(-k))
+        act((zb, 0, 143), ("w2", 0, 143), AF.Relu, m, nm)
+    act(("w1", 0, 512), ("io", 0, 512), AF.Abs, PM, -1.0)
+    act(("dmj", 0, 512), ("w1", 0, 512), AF.Relu, 1.0, -1.0)
+    act(("seg", 0, 512), ("io", 0, 512), AF.Sign)
+    act(("w3", 0, 128), ("Y", 0, 128), AF.Abs)
+    act(("ident", 0, 128), ("w3", 0, 128), AF.Relu, 1.0, -1.0)
+    act(("idm", 0, 128), ("ident", 0, 128), AF.Identity, 0.0, -6400.0)
+    act(("id8", 0, 128), ("ident", 0, 128), AF.Identity, 0.0, -float(Z0))
     copy(("mg16", 0, 32), ("mgI", 0, 32))
     ts(("damI", 512, 520), ("mgI", 16, 24), 6400.0, ALU.add)
     ts(("damI", 520, 528), ("mgI", 8, 16), 6400.0, ALU.add)
     A144 = (0, 144)
     ts(("EI",) + A144, ("damI", 384, 528), -6400.0, ALU.add, 0.0, ALU.max)
     ts(("AI",) + A144, ("EI",) + A144, 15, ALU.bitwise_and)
-    ts(("EF",) + A144, ("AI",) + A144, 3071.0, ALU.mult)
+    ts(("EF",) + A144, ("AI",) + A144, 3071.0, ALU.mult, 128.0, ALU.add)
     tt(("EG",) + A144, ("EF",) + A144, ("EI",) + A144, ALU.add)
-    ts(("pos16",) + A144, ("EG",) + A144, 0.0625, ALU.mult)
+    ts(("pp",) + A144, ("damI", 384, 528), 6400.0, ALU.is_ge)
+    ts(("qq",) + A144, ("damI", 384, 528), 9472.0, ALU.is_ge)
+    tt(("is2",) + A144, ("pp",) + A144, ("qq",) + A144, ALU.subtract)
+    tt(("EM",) + A144, ("EG",) + A144, ("is2",) + A144, ALU.mult)
+    ts(("pos16",) + A144, ("EM",) + A144, 0.0625, ALU.mult)
     copy(T1, ("aimI", 0, 1))
 
     def y_chunk(k):
@@ -255,70 +281,51 @@ def rank_program(g, core, T, topo):
         return (n, 0, 128)
 
     y_chunk(0)
-    ts(("dmj", 0, 512), ("io", 0, 512), PM, ALU.is_equal)
-    ts(("dm", 0, 16), ("io", 0, 16), PM, ALU.is_equal)
-    ts(("i16", 0, 16), ("io", 0, 16), 0.0625, ALU.mult)
-    ts(("nm", 0, 256), ("dmj", 0, 256), -1.0e9, ALU.mult, 1.0e9, ALU.add)
-    ts(("ZS", 0, 143), ("Y", 0, 143), float(15 - s2), ALU.is_equal, PS2, ALU.mult)
-    ts(("ZD", 0, 143), ("Y", 0, 143), float(15 - d2), ALU.is_equal, PD2, ALU.mult)
-    ts(("dmo", 0, 16), ("dm", 0, 16), OWN, ALU.mult)
     y_chunk(1)
-    ts(("dmh", 0, 16), ("dmo", 0, 16), 0.5, ALU.mult)
-    fill(("tabA", 0, Z0), 0.0)
-    fill(("tabB", 0, Z0), 0.0)
     y_chunk(2)
     ts(("gs", 0, 128), (("trI", 0, 3072), ("mg16", 0, 8)), T1, ALU.subtract)
     ship("gs", 0, 128, "y1", 3072, 3200, "a_g0")
-    half = ("seg", 512, 1024)
-    iota(half, [[0, 512]], 1, 0)
-    op("G", lambda: g.affine_select(ap(half), ap(half), [[0, 32], [1, 16]], ALU.not_equal, 0.0, 0, 0), [half], [half])
-    iota(("zero", 0, 512), [[0, 512]], 0, 0)
     y_chunk(3)
     copy(("sire16", 0, 192), ("sireI", 0, 192))
     copy(("dam16", 0, 192), ("damI", 0, 192))
-    ts(("ident", 0, 128), ("Y", 0, 128), 0.0, ALU.is_equal)
-    for y, m in ((0, Y0), (1, Y1)):
-        for h in range(2):
-            ts(("R%d%d" % (y, h), 0, 128), ("Y", 0, 128), 16.0 * (h - y), ALU.is_equal, m, ALU.mult)
     dma("S", [(T.trI[r:128:16, 0:3072], T.sire[:, 192:384]) for r in own], "l_tr", [], [("trI", 0, 3072)])
     for k in range(4):
         act(("FH", 768 * k, 768 * k + 768), ("y1", 768 * k, 768 * k + 768), AF.Abs, 0.0, 0.5)
 
     c = ("damI", 384, 512)
-    ts(f("q1"), c, 6272.0, ALU.is_lt)
-    ts(f("pp"), c, 6400.0, ALU.is_ge)
-    ts(f("qq"), c, 9472.0, ALU.is_ge)
-    ts(f("k1"), c, 6272.0, ALU.is_ge, 128.0, ALU.mult)
-    tt(f("is2"), f("pp"), f("qq"), ALU.subtract)
-    tt(f("xs"), f("q1"), c, ALU.mult)
-    tt(f("r1"), f("k1"), c, ALU.add)
-    ts(f("q3"), f("qq"), -3072.0, ALU.mult)
-    copy(("CF", 2048, 2304), (("W", 0, 3152), ("pos16", 128, 144)))
+    ts(f("mn"), c, 6400.0, ALU.min)
+    ts(f("x1"), c, -9472.0, ALU.add, 0.0, ALU.max)
+    ts(("tabA", Z0, Z0 + VD), ("FH", 0, VD), 2.0, ALU.mult)
+    copy(("CF", 2048, 2304), (("W", 0, WW), ("pos16", 128, 144)))
     mm(("pC", 0, 128), ("bs1", 0, 128), ("CF", 2176, 2304))
     mm(("pC", 128, 256), ("bd1", 0, 128), ("CF", 2176, 2304))
     mm(("pC", 256, 384), ("bs2", 0, 128), ("CF", 2048, 2176))
     mm(("pC", 384, 512), ("bd2", 0, 128), ("CF", 2048, 2176))
-    copy(("CF", 0, 1024), (("W", 0, 3152), ("pos16", 0, 64)))
+    copy(("CF", 0, 1024), (("W", 0, WW), ("pos16", 0, 64)))
     tt(("mk", 0, 512), ("pC", 0, 512), ("dmj", 0, 512), ALU.mult)
     scan(("msc", 0, 512), ("seg", 0, 512), ("mk", 0, 512), 0.0, ALU.mult, ALU.add)
     copy(("ms16", 0, 32), ("msc", 15, 512, 16))
     MS1, MD1, MS2, MD2 = [("ms16", 8 * k, 8 * k + 8) for k in range(4)]
 
-    def to_list(pb, z, flat, f0, o0):
+    def to_list(pb, z, flat, f0, o0, more=()):
         for i in range(16):
-            mm((pb, o0, o0 + 64), (z, 15 - i, 143 - i), (flat, f0 + i, f0 + 1024, 16), i == 0, i == 15)
+            mm((pb, o0, o0 + 64), (z, 15 - i, 143 - i), (flat, f0 + i, f0 + 1024, 16), i == 0, i == 15 and not more)
+        for k, (w, x) in enumerate(more):
+            mm((pb, o0, o0 + 64), (w, 0, 128), (x, o0, o0 + 64), False, k == len(more) - 1)
 
-    to_list("pS", "ZS", "CF", 0, 0)
-    to_list("pD", "ZD", "CF", 0, 0)
+    def list_s(h):
+        to_list("pS", "ZS", "CF", 1024 * h, 64 * h, (("ident", "mn"), ("idm", "pp"), ("id8", "qq")))
+
+    def list_d(h):
+        to_list("pD", "ZD", "CF", 1024 * h, 64 * h, (("ident", "mn"), ("ident", "x1"), ("idm", "is2")))
 
     def u_lists(h):
         v = lambda n: (n, 64 * h, 64 * h + 64)
-        tt(v("lS2"), v("is2"), v("pS"), ALU.mult)
-        tt(v("lD2"), v("is2"), v("pD"), ALU.mult)
-        tt(v("lS"), v("lS2"), v("PS"), ALU.add)
-        tt(v("lD"), v("lD2"), v("PD"), ALU.add)
-        copy(v("US16"), v("lS"))
-        copy(v("UD16"), v("lD"))
+        ts(v("US16"), v("pS"), float(Z0), ALU.add)
+        copy(v("UD16"), v("pD"))
+
+    list_s(0)
+    list_d(0)
 
     PART = [0]
     for n in (512, 768, 896, 896):
@@ -345,11 +352,8 @@ def rank_program(g, core, T, topo):
 
     def ghosts2(r, tab):
         o = 384 + 128 * r
-        tt(("gs", o, o + 128), ((tab, Z0, G1X), MD2), ("gt", 384 + 128 * (r - 1), 384 + 128 * r), ALU.add)
+        tt(("gs", o, o + 128), ((tab, Z0, E1), MD2), ("gt", 384 + 128 * (r - 1), 384 + 128 * r), ALU.add)
         ship("gs", o, o + 128, tab, G2X, G2X + 128, "a_g2%d" % r)
-
-    def double1(tab):
-        act((tab, G1X, G1X + 128), (tab, G1, G1 + 128), AF.Identity, 0.0, 2.0)
 
     def double3(tab):
         act((tab, X3, X3 + 1024), ("G3", 0, 1024), AF.Identity, 0.0, 0.5)
@@ -365,40 +369,40 @@ def rank_program(g, core, T, topo):
     sires1(2)
     act(("FH", 3072, 3200), ("y1", 3072, 3200), AF.Abs, 0.0, 0.5)
     dams1(tab, 0)
+    act(("dmo", 0, 16), ("dmj", 0, 16), AF.Identity, 0.0, OWN)
+    act(("dmh", 0, 16), ("dmj", 0, 16), AF.Identity, 0.0, HOWN)
+    act(("i16", 0, 16), ("io", 0, 16), AF.Identity, 0.0, 0.0625)
+    act(("nm", 0, 256), ("dmj", 0, 256), AF.Identity, 1.0e9, -1.0e9)
     ghosts1_act(1)
     ghosts1(1, tab)
     dams1(tab, 1)
     sires1(3)
-    act((tab, Z0, Z0 + 3200), ("y1", 0, 3200), AF.Abs)
+    act((tab, Z0 + VD, Z0 + 3200), ("y1", VD, 3200), AF.Abs)
     dams1(tab, 2)
     dams1(tab, 3)
-    REST = [(CUT + 512 * k, CUT + 512 * k + 512, pb) for k, pb in enumerate(("pA", "pB", "pE"))]
+    REST = [(CUT + 512 * k, CUT + 512 * k + 512, pb) for k, pb in enumerate(("pA", "pB"))]
+    HALF = [(0, CUT // 2), (CUT // 2, CUT)]
     copy(("sire16", 192, 384), ("sireI", 192, 384))
     copy(("dam16", 192, 384), ("damI", 192, 384))
-    for n, (a, b, pb) in enumerate(REST):
-        if n == 1:
-            act(("tmp", 0, CUT), ((tab, Z0, OWN1), ("sire16", 192, 192 + CUT // 16)), AF.Identity)
-            ghosts2_act(1, tab)
+    for a, b in HALF:
+        act(("tmp", a, b), ((tab, Z0, OWN1), ("sire16", 192 + a // 16, 192 + b // 16)), AF.Identity)
+    ghosts2_act(1, tab)
+    for a, b, pb in REST:
         act(("tmp", a, b), ((tab, Z0, OWN1), ("sire16", 192 + a // 16, 192 + b // 16)), AF.Identity)
         mm((pb, 0, 512), ("ident", 0, 128), ("tmp", a, b), True, False)
-    double1(tab)
     for a, b, pb in REST:
-        act(("tmp2", a - CUT, b - CUT), ((tab, Z0, G1X), ("dam16", 192 + a // 16, 192 + b // 16)), AF.Identity)
+        act(("tmp2", a - CUT, b - CUT), ((tab, Z0, E1), ("dam16", 192 + a // 16, 192 + b // 16)), AF.Identity)
         mm((pb, 0, 512), ("ident", 0, 128), ("tmp2", a - CUT, b - CUT), False, True)
-    tt(f("w8"), f("q1"), f("is2"), ALU.add)
-    ts(f("n2"), f("is2"), -1.0, ALU.mult, 1.0, ALU.add)
-    tt(f("r2"), f("r1"), f("q3"), ALU.add)
-    ts(f("lS"), f("w8"), float(Z0), ALU.mult)
-    tt(f("PD"), f("r2"), f("n2"), ALU.mult)
-    tt(f("PS"), f("xs"), f("lS"), ALU.add)
-    copy(("CF", 1024, 2048), (("W", 0, 3152), ("pos16", 64, 128)))
-    dma("S", [(T.W[q:128:16, 0:3072], T.sire[:, 0:192]) for q in own[1:]], "l_w2", [], [("W", 0, 3072)])
-    u_lists(0)
-    tt(("D2", 0, CUT), ((tab, Z0, G1X), ("dam16", 192, 192 + CUT // 16)), ("tmp", 0, CUT), ALU.add)
+    copy(("CF", 1024, 2048), (("W", 0, WW), ("pos16", 64, 128)))
+    dma("S", [(T.W[q:128:16, 8:WW], T.sire[:, 0:192]) for q in own[1:]], "l_w2", [], [("W", 8, WW)])
+    for a, b in HALF:
+        tt(("D2", a, b), ((tab, Z0, E1), ("dam16", 192 + a // 16, 192 + b // 16)), ("tmp", a, b), ALU.add)
     ghosts2(1, tab)
-    to_list("pS", "ZS", "CF", 1024, 64)
-    to_list("pD", "ZD", "CF", 1024, 64)
-    act(("T3", 0, 1024), ((tab, 0, OWN1), ("US16", 0, 64)), AF.Identity, KB)
+    u_lists(0)
+    act(("T3", 0, 1024), ((tab, 0, E1), ("US16", 0, 64)), AF.Identity, KB)
+    act(("T4", 0, KP), ((tab, Z0, X3), ("UD16", 0, KP // 16)), AF.Identity)
+    mm(("pC", 0, KP), ("ident", 0, 128), ("T3", 0, KP), True, False)
+    mm(("pC", 0, KP), ("ident", 0, 128), ("T4", 0, KP), False, True)
     JL, JB = [("cl", k, k + 1) for k in (0, 1)], [("cl", k, k + 1) for k in (2, 3)]
     scan(("tmp", 0, CUT), ("D2", 0, CUT), ("D2", 0, CUT), 0.0, ALU.max, ALU.max)
     scan(("FH", 0, CUT), ("D2", 0, CUT), ("D2", 0, CUT), 1.0e9, ALU.min, ALU.min)
@@ -411,6 +415,12 @@ def rank_program(g, core, T, topo):
                 ts(("off16", 0, 16), ("i16", 0, 16), K, ALU.add, 16.0, ALU.mult)
                 tt(("mk", 0, 256), (("tmp", 0, 3072), ("off16", 0, 16)), ("nm", 0, 256), ALU.max)
                 act(("junk", 0, 256), ("mk", 0, 256), AF.Sign, LAST, -1.0, K2)
+    act(("seg", 512, 1024), ("io", 0, 512), AF.Sign)
+    for k in (-1, 0, 1):
+        act(("w3", 0, 128), ("Y", 0, 128), AF.Abs, float(-16 * k))
+        for y, m, nm in ((0, Y0, NY0), (1, Y1, NY1)):
+            if 0 <= y + k < 2:
+                act(("R%d%d" % (y, y + k), 0, 128), ("w3", 0, 128), AF.Relu, m, nm)
     ts(JL[0], K, 16.0, ALU.mult, K2, ALU.add)
     act(("junk", 0, 3072), ("FH", 0, 3072), AF.Sign, ("FH", 3071, 3072), -1.0, JB[0])
 
@@ -437,35 +447,33 @@ def rank_program(g, core, T, topo):
         ts(("sm16", 16, 17), ("ci", 17, 18), 191.9375, ALU.mult, ("cl", 16, 17), ALU.add)
         tt(("lk", 0, 16), (("trI", 0, 3072), ("sm16", 16, 17)), ("dmo", 0, 16), ALU.mult)
         red(("cl", 17, 18), ("lk", 0, 16))
-        tt(("lk", 16, 32), (("W", 0, 3152), founder_a(("cl", 17, 18), 20)), ("dmo", 0, 16), ALU.mult)
+        tt(("lk", 16, 32), (("W", 8, WW), founder_a(("cl", 17, 18), 20)), ("dmo", 0, 16), ALU.mult)
         red(("cl", 23, 24), ("lk", 16, 32))
         tt(("lk", 32, 48), (("y1", 0, 3072), founder_b(20)), ("dmh", 0, 16), ALU.mult)
         red((land, 4 * rank, 4 * rank + 1), ("lk", 32, 48))
 
     def best_lines_a():
-        copy(("bg2", 0, 16), (("W", 0, 3152), founder_a(("bsc", 15, 16), 32)))
+        copy(("bg2", 0, 16), (("W", 8, WW), founder_a(("bsc", 15, 16), 32)))
         mm(("pM", 288, 304), ("bs1", 0, 128), ("bg2", 0, 16))
 
     def best_lines_b():
-        tt(("bm2", 0, 16), ("pM", 288, 304), ("dm", 0, 16), ALU.mult)
+        tt(("bm2", 0, 16), ("pM", 288, 304), ("dmj", 0, 16), ALU.mult)
         red(("cl", 35, 36), ("bm2", 0, 16))
-        ts(("yt16", 0, 16), (("y1", 0, 3072), founder_b(32)), 65536.0, ALU.add)
+        copy(("yt16", 0, 16), (("y1", 0, 3072), founder_b(32)))
 
     def chain2(land):
         copy(("sm16", 40, 41), JL[1])
-        tt(("lk", 48, 64), (("sf", 0, 1024), ("sm16", 40, 41)), ("dm", 0, 16), ALU.mult)
-        red(("cl", 40, 41), ("lk", 48, 64))
-        ts(("lk", 64, 80), ("bT", 0, 16), ("cl", 40, 41), ALU.is_equal)
-        tt(("lk", 80, 96), ("lk", 64, 80), ("yt16", 0, 16), ALU.mult)
-        red(("cl", 41, 42), ("lk", 80, 96), ALU.max)
-        ts((land, 4 * rank, 4 * rank + 1), ("cl", 41, 42), -65536.0, ALU.add, HOWN, ALU.mult)
+        tt(("lk", 48, 64), (("sy", 0, 1024), ("sm16", 40, 41)), ("dmh", 0, 16), ALU.mult)
+        red((land, 4 * rank, 4 * rank + 1), ("lk", 48, 64))
 
     chain1("land1")
     share_aim("land1", "a_aim1")
-    tt(("key", 0, 1024), ((tab, Z0, X3), ("UD16", 0, 64)), ("T3", 0, 1024), ALU.add)
+    tt(("key", KP, 1024), ((tab, Z0, X3), ("UD16", KP // 16, 64)), ("T3", KP, 1024), ALU.add)
 
-    def rows_a(between):
-        op("V", lambda: g.vector.transpose(T.D2[:, 1024:2048], T.key[:, 0:1024]), [("key", 0, 1024)], [("D2", 1024, 2048)])
+    def rows_a(k, between):
+        turn(("D2", 1024 + k, 2048), ("key", k, 1024))
+        if k:
+            turn(("D2", 1024, 1024 + k), ("pC", 0, k))
         between()
         scan(("D2", 0, 1024), ("seg", 0, 1024), ("D2", 1024, 2048), 0.0, ALU.mult, ALU.max)
 
@@ -483,28 +491,31 @@ def rank_program(g, core, T, topo):
 
     def best_a(r):
         k = 16 * (r - 1)
-        ts(("bR", k, k + 16), ("dm", 0, 16), JB[r - 1], ALU.mult, -1.0, ALU.mult)
+        ts(("bR", k, k + 16), ("dmj", 0, 16), JB[r - 1], ALU.mult, -1.0, ALU.mult)
         mm(("pY", 128 + k, 144 + k), ("blk", 0, 128), ("bR", k, k + 16))
 
     def best_b(r):
         k = 16 * (r - 1)
         copy(("bT", k, k + 16), ("pY", 128 + k, 144 + k))
 
+    def sire_act(r, a=0, b=1024):
+        k = 64 * (r - 1)
+        act(("sf", 16 * k + a, 16 * k + b), (("bT", 16 * (r - 1), 16 * r), ("row16", k + a // 16, k + b // 16)), AF.Identity)
+
     def sire_cols(r):
-        act(("sf", 1024 * (r - 1), 1024 * r), (("bT", 16 * (r - 1), 16 * r), ("row16", 64 * (r - 1), 64 * r)), AF.Identity)
-        to_list("pY", "ZS", "sf", 1024 * (r - 1), 64 * (r - 1))
+        to_list("pE", "ZS", "sf", 1024 * (r - 1), 64 * (r - 1))
 
     BH = [("cl", 4, 5), ("cl", 5, 6)]
 
     def outputs(r, first):
-        ts(("yso", 64 * (r - 1), 64 * r), ("pY", 64 * (r - 1), 64 * r), float(first), ALU.add)
+        ts(("yso", 64 * (r - 1), 64 * r), ("pE", 64 * (r - 1), 64 * r), float(first), ALU.add)
         ts(("yto", r - 1, r), BH[r - 1], 2.0, ALU.mult, T1, ALU.add)
 
     def aims(r, land):
         op("V", lambda: g.vector.tensor_reduce(ap(BH[r - 1]), T[land][:, 0:16:4], AxisListType.X, ALU.add),
            [(land, 0, 16)], [BH[r - 1]])
 
-    rows_a(lambda: aims(1, "land1"))
+    rows_a(KP, lambda: aims(1, "land1"))
     rows_b()
     n = 48
     best_a(1)
@@ -514,9 +525,10 @@ def rank_program(g, core, T, topo):
     rows_c(0)
     ts(("ci", n + 1, n + 2), ("ci", n + 2, n + 3), 15, ALU.bitwise_and)
     ts(("sm16", n, n + 1), ("ci", n + 1, n + 2), 191.9375, ALU.mult, ("cl", n + 1, n + 2), ALU.add)
-    copy(("bg", 0, 16), (("W", 0, 3152), ("sm16", n, n + 1)))
+    copy(("bg", 0, 16), (("W", 8, WW), ("sm16", n, n + 1)))
     mm(("pM", 256, 272), ("bs2", 0, 128), ("bg", 0, 16))
     mm(("pM", 272, 288), ("bd2", 0, 128), ("bg", 0, 16))
+    list_s(1)
     best_b(1)
     tt(("bm", 0, 32), ("pM", 256, 288), ("dmj", 0, 32), ALU.mult)
     scan(("bsc", 0, 32), ("seg", 0, 32), ("bm", 0, 32), 0.0, ALU.mult, ALU.add)
@@ -538,42 +550,48 @@ def rank_program(g, core, T, topo):
                 ghosts1(r, tab)
                 if r == 2:
                     best_lines_a()
+                    list_d(1)
         act((tab, Z0 + 800 * nv, Z0 + 3200), ("FH", 800 * nv, 3200), AF.Identity, 0.0, 2.0)
+        if r == 3:
+            sire_act(2, 0, 512)
         ghosts2_act(r, tab)
         copy(("ub1", 0, 16), ((tab, Z0, OWN1), BS))
-        tt(("Ub", 0, 16), ((tab, Z0, G1X), BD), ("ub1", 0, 16), ALU.add)
+        tt(("Ub", 0, 16), ((tab, Z0, E1), BD), ("ub1", 0, 16), ALU.add)
         ghosts2(r, tab)
         if r == 2:
             best_lines_b()
+        else:
+            outputs(1, 6400)
         for k in range(2):
             a, b = 512 * k, 512 * k + 512
             act(("tmp2", a, b), (("Ub", 0, 16), ("row16", 32 * k, 32 * k + 32)), AF.Identity)
-            tt(("T3", a, b), ((tab, 0, OWN1), ("US16", 32 * k, 32 * k + 32)), ("tmp2", a, b), ALU.add)
-        double1(tab)
+            tt(("T3", a, b), ((tab, 0, E1), ("US16", 32 * k, 32 * k + 32)), ("tmp2", a, b), ALU.add)
         if r == 2:
             u_lists(1)
-            sire_cols(1)
-        act(("T4", 0, 1024), ((tab, 0, OWN1), ("US16", 64, 128)), AF.Identity, KB if r == 2 else 0.0)
-        if r == 3:
+            act(("sy", 0, 1024), (("yt16", 0, 16), ("row16", 0, 64)), AF.Identity)
+        else:
+            sire_act(2, 512, 1024)
             sire_cols(2)
+        act(("T4", 0, 1024), ((tab, 0, E1), ("US16", 64, 128)), AF.Identity, KB if r == 2 else 0.0)
         tt(("G3", 0, 1024), ((tab, Z0, X3), ("UD16", 0, 64)), ("T3", 0, 1024), ALU.add)
 
     tab = "tabB"
     begin(2, tab)
-    scan(("tmp", 0, 1024), ("G3", 0, 1024), ("G3", 0, 1024), 0.0, ALU.max, ALU.max)
-    act(("junk", 0, 1024), ("tmp", 0, 1024), AF.Sign, ("tmp", 1023, 1024), -1.0, JL[1])
-    double3(tab)
     ghosts3(2, tab)
+    scan(("tmp", 0, 1024), ("G3", 0, 1024), ("G3", 0, 1024), 0.0, ALU.max, ALU.max)
+    double3(tab)
+    act(("junk", 0, 1024), ("tmp", 0, 1024), AF.Sign, ("tmp", 1023, 1024), -1.0, JL[1])
     scan(("FH", 0, 1024), ("G3", 0, 1024), ("G3", 0, 1024), 1.0e9, ALU.min, ALU.min)
     act(("junk", 0, 1024), ("FH", 0, 1024), AF.Sign, ("FH", 1023, 1024), -1.0, JB[1])
+    sire_act(1)
     chain2("land2")
     share_aim("land2", "a_aim2")
     tt(("key", 0, 1024), ((tab, Z0, TW), ("UD16", 64, 128)), ("T4", 0, 1024), ALU.add)
-    rows_a(lambda: aims(2, "land2"))
+    rows_a(0, lambda: aims(2, "land2"))
     rows_b()
     best_a(2)
+    sire_cols(1)
     ts(("sm16", 58, 59), JB[1], -1.0, ALU.mult)
-    outputs(1, 6400)
     rows_c(64)
     best_b(2)
 
@@ -591,7 +609,7 @@ def rank_program(g, core, T, topo):
         tt(("key", a, b), ((tab, Z0, TW), ("UD16", 64 + a // 16, 64 + b // 16)), ("T3", a, b), ALU.add)
         act(("yo", 1024 + a, 1024 + b), ("key", a, b), AF.Identity, 65535.0, -0.25)
         dma("S", [(T.yf[:, 1024 + a:1024 + b], T.yo[:, 1024 + a:1024 + b])], "o_f4%s" % "abc"[k], [("yo", 1024 + a, 1024 + b)], [])
-        if k == 0:
+        if k == 1:
             outputs(2, 9600)
             dma("S", [(T.ys[:], T.yso[:])], "o_ys", [("yso", 0, 128)], [])
             dma("S", [(T.yt[:], T.yto[:])], "o_yt", [("yto", 0, 2)], [])

from concourse.bass import DstId, RemoteDMATransfer
from concourse.mybir import AluOpType, AxisListType, ActivationFunctionType

ALU = AluOpType
AF = ActivationFunctionType
F32, I32, U16, B16 = "float32", "int32", "uint16", "bfloat16"
Z0 = 8
OWN1 = Z0 + 6272
G1 = Z0 + 6272
E1 = Z0 + 6400
G2X = Z0 + 6400
X3 = Z0 + 6528
G3X = Z0 + 7552
TW = Z0 + 7680
WW = 3080
KP = 512
VD = 1024
CUT = 2048


def _sb(n, d=F32):
    return ("sbuf", [128, n], d)


SCRATCH = {
    "sireI": _sb(384, I32), "damI": _sb(528, I32), "mgI": _sb(32, I32), "aimI": _sb(1, I32),
    "trI": _sb(3072, I32), "W": _sb(WW, I32),
    "y1": _sb(3200), "FH": _sb(3200), "tabA": _sb(TW), "tabB": _sb(TW),
    "tmp": _sb(3072), "tmp2": _sb(1024), "D2": _sb(2048), "DT": _sb(1024), "KS": _sb(1024), "CF": _sb(2304),
    "T3": _sb(1024), "T4": _sb(1024), "key": _sb(1024), "G3": _sb(1024),
    "yo": _sb(2048), "sf": _sb(2048), "sy": _sb(1024), "seg": _sb(1024), "zero": _sb(512),
    "io": _sb(512), "dmj": _sb(512), "mk": _sb(512), "msc": _sb(512), "junk": _sb(3072, B16),
    "Y": _sb(143), "Gm": _sb(128), "blk": _sb(128), "bs1": _sb(128), "bd1": _sb(128), "bs2": _sb(128), "bd2": _sb(128),
    "ident": _sb(128), "idm": _sb(128), "id8": _sb(128), "ZS": _sb(143), "ZD": _sb(143),
    "w1": _sb(512), "w2": _sb(144), "w3": _sb(128),
    "R00": _sb(128, B16), "R01": _sb(128, B16), "R10": _sb(128, B16), "R11": _sb(128, B16),
    "pI": _sb(8, I32), "cc": _sb(32), "dmo": _sb(16), "dmh": _sb(16),
    "sire16": _sb(384, U16), "dam16": _sb(384, U16), "mg16": _sb(32, U16), "ms16": _sb(32, U16),
    "pos16": _sb(144, U16), "US16": _sb(128, U16), "UD16": _sb(128, U16), "row16": _sb(128, U16), "sm16": _sb(64, U16),
    "EI": _sb(144, I32), "AI": _sb(144, I32), "EF": _sb(144), "EG": _sb(144), "EM": _sb(144),
    "pp": _sb(144), "qq": _sb(144), "is2": _sb(144), "mn": _sb(128), "x1": _sb(128),
    "gs": _sb(1152), "gt": _sb(768), "ri": _sb(64, I32), "rb": _sb(64, I32), "rbf": _sb(64, B16),
    "bT": _sb(32), "bR": _sb(32), "bg": _sb(16), "bm": _sb(32), "bsc": _sb(32), "Ub": _sb(16), "ub1": _sb(16), "HB": _sb(16),
    "cl": _sb(64), "ci": _sb(64, I32), "lk": _sb(128), "land1": _sb(16), "land2": _sb(16),
    "off16": _sb(16, U16), "i16": _sb(16), "nm": _sb(256), "bg2": _sb(16), "bm2": _sb(16), "yt16": _sb(16),
    "yso": _sb(128), "yto": _sb(2),
}
del SCRATCH["DT"], SCRATCH["KS"]
BANKS = ("pC", "pS", "pD", "pM", "pY", "pA", "pB", "pE")
for _b in BANKS:
    SCRATCH[_b] = ("psum", [128, 512], F32)
SEMAPHORES = ["qV", "qA", "qP", "qG", "sent", "l_sire", "l_sire2", "l_dam0", "l_dam1", "l_dam2", "l_mg", "l_aim",
              "l_t0", "l_t1", "l_t2", "l_t3", "l_w", "l_w2", "l_tr", "o_ys", "o_yt", "o_f3", "o_f4a", "o_f4b", "o_f4c",
              "a_g0", "a_g11", "a_g12", "a_g13", "a_g21", "a_g22", "a_g23", "a_g32", "a_g33", "a_aim1", "a_aim2"]


def rank_program(g, core, T, topo):
    rank = T.rank_of(core)
    if rank is None:
        return
    N = len(T.cores)
    nxt = T.cores[(rank + 1) % N]
    Q = {"V": g.vector, "A": g.scalar, "P": g.tensor, "G": g, "S": g.sync}
    SEM = {"V": "qV", "A": "qA", "P": "qP", "G": "qG"}
    cnt = {"V": 0, "A": 0, "P": 0, "G": 0}
    known = {e: {} for e in Q}
    recs = {}
    clocks = {}
    total = {}

    def need(e, reads, writes, acc=False):
        req = {}
        for kind, regs in ((0, reads), (1, writes)):
            for b, c0, c1 in regs:
                for o0, o1, ow, sem, val, oe in recs.get(b, []):
                    if o1 <= c0 or o0 >= c1 or (kind == 0 and not ow) or (oe == e and acc):
                        continue
                    req[sem] = max(req.get(sem, 0), val)
        live = {s: v for s, v in req.items() if known[e].get(s, 0) < v}
        for s in sorted(live):
            if any(o != s and clocks.get((o, live[o]), {}).get(s, 0) >= live[s] for o in live):
                continue
            Q[e].wait_ge(T.sem[s], live[s])
        for s, v in live.items():
            known[e][s] = max(known[e].get(s, 0), v)
            for o, w in clocks.get((s, v), {}).items():
                known[e][o] = max(known[e].get(o, 0), w)

    def note(e, reads, writes, sem, val):
        clocks[(sem, val)] = dict(known[e]) if e in known else {}
        total[sem] = val
        for b, c0, c1 in writes:
            keep = [r for r in recs.get(b, []) if not (c0 <= r[0] and r[1] <= c1)]
            keep.append((c0, c1, True, sem, val, e))
            recs[b] = keep
        for b, c0, c1 in reads:
            keep = [r for r in recs.get(b, []) if not (not r[2] and r[5] == e and c0 <= r[0] and r[1] <= c1)]
            keep.append((c0, c1, False, sem, val, e))
            recs[b] = keep

    def reg(x):
        return (x[0], 0, 512) if x[0] in BANKS else (x[0], x[1], x[2])

    def ap(x):
        if len(x) == 4:
            return T[x[0]][:, x[1]:x[2]:x[3]]
        return T[x[0]][:, x[1]:x[2]]

    def op(e, fn, reads, writes, acc=False):
        rd, wr = [reg(x) for x in reads], [reg(x) for x in writes]
        need(e, rd, wr, acc)
        cnt[e] += 1
        fn().then_inc(T.sem[SEM[e]], 1)
        note(e, rd, wr, SEM[e], cnt[e])

    def src(x):
        if len(x) == 2:
            return ap(x[0]).indirect(ap(x[1])), [x[0], x[1]]
        return ap(x), [x]

    def copy(out, a):
        s, rd = src(a)
        op("V", lambda: g.vector.tensor_copy(ap(out), s), rd, [out])

    def tt(out, a, b, alu):
        s, rd = src(a)
        op("V", lambda: g.vector.tensor_tensor(ap(out), s, ap(b), alu), rd + [b], [out])

    def ts(out, a, s1, o1, s2=None, o2=None):
        s, rd = src(a)
        v1 = ap(s1) if isinstance(s1, tuple) else s1
        v2 = ap(s2) if isinstance(s2, tuple) else s2
        rd = rd + [x for x in (s1, s2) if isinstance(x, tuple)]
        if o2 is None:
            op("V", lambda: g.vector.tensor_scalar(ap(out), s, v1, None, o1), rd, [out])
        else:
            op("V", lambda: g.vector.tensor_scalar(ap(out), s, v1, v2, o1, o2), rd, [out])

    def red(out, a, alu=ALU.add):
        op("V", lambda: g.vector.tensor_reduce(ap(out), ap(a), AxisListType.X, alu), [a], [out])

    def fill(a, v):
        op("V", lambda: g.vector.memset(ap(a), v), [], [a])

    def turn(out, a):
        op("V", lambda: g.vector.transpose(ap(out), ap(a)), [a], [out])

    def scan(out, d0, d1, init, o0, o1):
        iv = ap(init) if isinstance(init, tuple) else init
        rd = [d0, d1] + ([init] if isinstance(init, tuple) else [])
        op("V", lambda: g.vector.tensor_tensor_scan(ap(out), ap(d0), ap(d1), iv, o0, o1), rd, [out])

    def act(out, a, func, bias=0.0, scale=1.0, accum=None):
        s, rd = src(a)
        bv = ap(bias) if isinstance(bias, tuple) else bias
        sv = ap(scale) if isinstance(scale, tuple) else scale
        rd = rd + [x for x in (bias, scale) if isinstance(x, tuple)]
        if accum is None:
            op("A", lambda: g.scalar.activation(ap(out), s, func, bias=bv, scale=sv), rd, [out])
        else:
            op("A", lambda: g.scalar.activation(ap(out), s, func, bias=bv, scale=sv, accum_out=ap(accum)), rd, [out, accum])

    def mm(out, lhsT, rhs, start=True, stop=True):
        op("P", lambda: g.tensor.matmul(ap(out), ap(lhsT), ap(rhs), start, stop), [lhsT, rhs], [out], acc=True)

    def iota(out, pattern, base, cm):
        if out[0] in ("pI", "W"):
            op("G", lambda: g.iota(ap(out), pattern, base, cm), [], [out])
        else:
            op("G", lambda: g.iota(ap(out), pattern, base, cm, allow_small_or_imprecise_dtypes=True), [], [out])

    def dma(e, pairs, sem, reads, writes):
        need(e, reads, writes)
        for o, i in pairs:
            Q[e].dma_start(o, i).then_inc(T.sem[sem], 16)
        note("D" + sem, reads, writes, sem, 16 * len(pairs))

    engs = [e for e in topo.engines(core, nxt) if all(e in topo.engines(core, c) for c in T.cores if c != core)]
    mask = sum(1 << e for e in engs)
    sent = [0]

    def ship(buf, a, b, out, oa, ob, sem):
        need("G", [(buf, a, b)], [])
        rid, pid, _ = topo.addr(nxt)
        g.remote_dma(out_ap=T[out][:, oa:ob], in_ap=T[buf][:, a:b], remote_sem=T.sem[sem], local_sem=T.sem.sent,
                     pid=pid, routing_id=rid, dma_engine_mask=mask)
        sent[0] += len(engs)
        note("R", [], [(out, oa, ob)], sem, len(engs))

    def share_aim(land, sem):
        need("G", [(land, 4 * rank, 4 * rank + 1)], [])
        others = [c for c in T.cores if c != core]
        ids = [DstId(rid=topo.addr(c)[0], pnc=topo.addr(c)[1]) for c in others]
        a = T[land][:, 4 * rank:4 * rank + 1]
        g.remote_dma_fused([RemoteDMATransfer(dst_ids=ids, dma_engine_mask=mask, remote_sem=T.sem[sem], srcs=[a],
                                              dsts=[a for c in others])], local_sem=T.sem.sent)
        sent[0] += len(engs)
        for k in range(N):
            if k != rank:
                note("R", [], [(land, 4 * k, 4 * k + 1)], sem, len(engs) * (N - 1))

    dma("A", [(T.damI[:, 384:512], T.dam[:, 384:512])], "l_dam1", [], [("damI", 384, 512)])
    dma("S", [(T.mgI[:], T.mg[:])], "l_mg", [], [("mgI", 0, 32)])
    dma("S", [(T.aimI[:], T.aim0[:])], "l_aim", [], [("aimI", 0, 1)])
    dma("A", [(T.trI[:, 0:768], T.trait[:, 0:768])], "l_t0", [], [("trI", 0, 768)])
    dma("A", [(T.trI[:, 768:1536], T.trait[:, 768:1536])], "l_t1", [], [("trI", 768, 1536)])
    dma("A", [(T.trI[:, 1536:2304], T.trait[:, 1536:2304])], "l_t2", [], [("trI", 1536, 2304)])
    dma("A", [(T.trI[:, 2304:3072], T.trait[:, 2304:3072])], "l_t3", [], [("trI", 2304, 3072)])
    dma("S", [(T.sireI[:, 0:192], T.sire[:, 0:192])], "l_sire", [("trI", 768, 1536)], [("sireI", 0, 192)])
    dma("S", [(T.damI[:, 0:192], T.dam[:, 0:192])], "l_dam0", [], [("damI", 0, 192)])
    iota(("pI", 0, 1), [[0, 1]], 0, 1)
    iota(("Gm", 0, 128), [[16, 8], [0, 16]], 0, 0)
    iota(("Y", 0, 143), [[1, 143]], 0, -1)
    iota(("io", 0, 512), [[0, 32], [1, 16]], 0, 0)
    iota(("W", 800, WW), [[0, WW - 800]], 0, 0)
    iota(("zero", 0, 512), [[0, 512]], 0, 0)
    iota(("tabA", 0, Z0), [[0, Z0]], 0, 0)
    iota(("tabB", 0, Z0), [[0, Z0]], 0, 0)
    fill(("W", 0, 800), 0)
    own = [4 * rank + k for k in range(4)]
    d1, s2, d2 = [(4 * rank + 4 + k) % 16 for k in range(3)]
    wp = [(T.W[own[0]:128:16, 8:WW], T.sire[:, 0:192])]
    wp.append((T.W[d1:128:16, 8:WW], T.dam[:, 0:192]))
    wp.append((T.W[s2:128:16, 8:WW], T.sire[:, 192:384]))
    wp.append((T.W[d2:128:16, 8:WW], T.dam[:, 192:384]))
    dma("S", wp, "l_w", [], [("W", 8, WW)])
    dma("S", [(T.sireI[:, 192:384], T.sire[:, 192:384])], "l_sire2", [], [("sireI", 192, 384)])
    dma("S", [(T.damI[:, 192:384], T.dam[:, 192:384])], "l_dam2", [], [("damI", 192, 384)])

    PM, PG, OWN, KB, PS1, PD1, PS2, PD2, Y0, Y1, T1, HOWN, NS2, ND2, NY0, NY1 = [("cc", k, k + 1) for k in range(16)]
    ts(("pI", 1, 2), ("pI", 0, 1), 15, ALU.bitwise_and)
    ts(("pI", 3, 4), ("pI", 0, 1), 16, ALU.bitwise_and, 4, ALU.logical_shift_right)
    copy(PM, ("pI", 1, 2))
    ts(("pI", 2, 3), ("pI", 1, 2), 2, ALU.logical_shift_right)
    copy(Y1, ("pI", 3, 4))
    tt(PG, ("pI", 0, 1), PM, ALU.subtract)
    ts(OWN, ("pI", 2, 3), float(rank), ALU.is_equal)
    ts(HOWN, ("pI", 2, 3), float(rank), ALU.is_equal, 0.5, ALU.mult)
    for col, r in ((PS1, own[0]), (PD1, d1), (PS2, s2), (PD2, d2)):
        ts(col, PM, float(r), ALU.is_equal)
    for col, r in ((NS2, s2), (ND2, d2)):
        ts(col, PM, float(r), ALU.is_equal, -1.0, ALU.mult)
    ts(KB, PM, -1.0 / 64, ALU.mult, 15.0 / 64, ALU.add)
    ts(Y0, Y1, -1.0, ALU.mult, 1.0, ALU.add)
    ts(NY1, Y1, -1.0, ALU.mult)
    ts(NY0, Y1, -1.0, ALU.add)
    act(("w3", 0, 128), ("Gm", 0, 128), AF.Abs, PG, -1.0)
    act(("blk", 0, 128), ("w3", 0, 128), AF.Relu, 1.0, -1.0)
    for b, col in (("bs1", PS1), ("bd1", PD1), ("bs2", PS2), ("bd2", PD2)):
        act((b, 0, 128), ("blk", 0, 128), AF.Identity, 0.0, col)
    for zb, k, m, nm in (("ZS", 15 - s2, PS2, NS2), ("ZD", 15 - d2, PD2, ND2)):
        act(("w2", 0, 143), ("Y", 0, 143), AF.Abs, float(-k))
        act((zb, 0, 143), ("w2", 0, 143), AF.Relu, m, nm)
    act(("w1", 0, 512), ("io", 0, 512), AF.Abs, PM, -1.0)
    act(("dmj", 0, 512), ("w1", 0, 512), AF.Relu, 1.0, -1.0)
    act(("seg", 0, 512), ("io", 0, 512), AF.Sign)
    act(("w3", 0, 128), ("Y", 0, 128), AF.Abs)
    act(("ident", 0, 128), ("w3", 0, 128), AF.Relu, 1.0, -1.0)
    act(("idm", 0, 128), ("ident", 0, 128), AF.Identity, 0.0, -6400.0)
    act(("id8", 0, 128), ("ident", 0, 128), AF.Identity, 0.0, -float(Z0))
    copy(("mg16", 0, 32), ("mgI", 0, 32))
    ts(("damI", 512, 520), ("mgI", 16, 24), 6400.0, ALU.add)
    ts(("damI", 520, 528), ("mgI", 8, 16), 6400.0, ALU.add)
    A144 = (0, 144)
    ts(("EI",) + A144, ("damI", 384, 528), -6400.0, ALU.add, 0.0, ALU.max)
    ts(("AI",) + A144, ("EI",) + A144, 15, ALU.bitwise_and)
    ts(("EF",) + A144, ("AI",) + A144, 3071.0, ALU.mult, 128.0, ALU.add)
    tt(("EG",) + A144, ("EF",) + A144, ("EI",) + A144, ALU.add)
    ts(("pp",) + A144, ("damI", 384, 528), 6400.0, ALU.is_ge)
    ts(("qq",) + A144, ("damI", 384, 528), 9472.0, ALU.is_ge)
    tt(("is2",) + A144, ("pp",) + A144, ("qq",) + A144, ALU.subtract)
    tt(("EM",) + A144, ("EG",) + A144, ("is2",) + A144, ALU.mult)
    ts(("pos16",) + A144, ("EM",) + A144, 0.0625, ALU.mult)
    copy(T1, ("aimI", 0, 1))

    def y_chunk(k):
        a, b = 768 * k, 768 * k + 768
        ts(("y1", a, b), ("trI", a, b), T1, ALU.subtract)

    def f(n):
        return (n, 0, 128)

    y_chunk(0)
    y_chunk(1)
    y_chunk(2)
    ts(("gs", 0, 128), (("trI", 0, 3072), ("mg16", 0, 8)), T1, ALU.subtract)
    ship("gs", 0, 128, "y1", 3072, 3200, "a_g0")
    y_chunk(3)
    copy(("sire16", 0, 192), ("sireI", 0, 192))
    copy(("dam16", 0, 192), ("damI", 0, 192))
    dma("S", [(T.trI[r:128:16, 0:3072], T.sire[:, 192:384]) for r in own], "l_tr", [], [("trI", 0, 3072)])
    for k in range(4):
        act(("FH", 768 * k, 768 * k + 768), ("y1", 768 * k, 768 * k + 768), AF.Abs, 0.0, 0.5)

    c = ("damI", 384, 512)
    ts(f("mn"), c, 6400.0, ALU.min)
    ts(f("x1"), c, -9472.0, ALU.add, 0.0, ALU.max)
    ts(("tabA", Z0, Z0 + VD), ("FH", 0, VD), 2.0, ALU.mult)
    copy(("CF", 2048, 2304), (("W", 0, WW), ("pos16", 128, 144)))
    mm(("pC", 0, 128), ("bs1", 0, 128), ("CF", 2176, 2304))
    mm(("pC", 128, 256), ("bd1", 0, 128), ("CF", 2176, 2304))
    mm(("pC", 256, 384), ("bs2", 0, 128), ("CF", 2048, 2176))
    mm(("pC", 384, 512), ("bd2", 0, 128), ("CF", 2048, 2176))
    copy(("CF", 0, 1024), (("W", 0, WW), ("pos16", 0, 64)))
    tt(("mk", 0, 512), ("pC", 0, 512), ("dmj", 0, 512), ALU.mult)
    scan(("msc", 0, 512), ("seg", 0, 512), ("mk", 0, 512), 0.0, ALU.mult, ALU.add)
    copy(("ms16", 0, 32), ("msc", 15, 512, 16))
    MS1, MD1, MS2, MD2 = [("ms16", 8 * k, 8 * k + 8) for k in range(4)]

    def to_list(pb, z, flat, f0, o0, more=()):
        for i in range(16):
            mm((pb, o0, o0 + 64), (z, 15 - i, 143 - i), (flat, f0 + i, f0 + 1024, 16), i == 0, i == 15 and not more)
        for k, (w, x) in enumerate(more):
            mm((pb, o0, o0 + 64), (w, 0, 128), (x, o0, o0 + 64), False, k == len(more) - 1)

    def list_s(h):
        to_list("pS", "ZS", "CF", 1024 * h, 64 * h, (("ident", "mn"), ("idm", "pp"), ("id8", "qq")))

    def list_d(h):
        to_list("pD", "ZD", "CF", 1024 * h, 64 * h, (("ident", "mn"), ("ident", "x1"), ("idm", "is2")))

    def u_lists(h):
        v = lambda n: (n, 64 * h, 64 * h + 64)
        ts(v("US16"), v("pS"), float(Z0), ALU.add)
        copy(v("UD16"), v("pD"))

    list_s(0)
    list_d(0)

    PART = [0]
    for n in (512, 768, 896, 896):
        PART.append(PART[-1] + n)

    def sires1(k):
        a, b = PART[k], PART[k + 1]
        act(("tmp", a, b), (("FH", 0, 3072), ("sire16", a // 16, b // 16)), AF.Identity)

    def dams1(tab, k):
        a, b = PART[k], PART[k + 1]
        tt((tab, Z0 + 3200 + a, Z0 + 3200 + b), (("FH", 0, 3200), ("dam16", a // 16, b // 16)), ("tmp", a, b), ALU.add)

    def ghosts1_act(r):
        act(("gt", 128 * r - 128, 128 * r), (("FH", 0, 3072), MS1), AF.Identity)

    def ghosts1(r, tab):
        o = 128 * r
        tt(("gs", o, o + 128), (("FH", 0, 3200), MD1), ("gt", o - 128, o), ALU.add)
        ship("gs", o, o + 128, tab, G1, G1 + 128, "a_g1%d" % r)

    def ghosts2_act(r, tab):
        act(("gt", 384 + 128 * (r - 1), 384 + 128 * r), ((tab, Z0, OWN1), MS2), AF.Identity)

    def ghosts2(r, tab):
        o = 384 + 128 * r
        tt(("gs", o, o + 128), ((tab, Z0, E1), MD2), ("gt", 384 + 128 * (r - 1), 384 + 128 * r), ALU.add)
        ship("gs", o, o + 128, tab, G2X, G2X + 128, "a_g2%d" % r)

    def double3(tab):
        act((tab, X3, X3 + 1024), ("G3", 0, 1024), AF.Identity, 0.0, 0.5)

    def ghosts3(r, tab):
        o = 896 + 128 * (r - 2)
        ts(("gs", o, o + 128), (("G3", 0, 1024), ("mg16", 24, 32)), 0.5, ALU.mult)
        ship("gs", o, o + 128, tab, G3X, G3X + 128, "a_g3%d" % r)

    tab = "tabA"
    sires1(0)
    sires1(1)
    sires1(2)
    act(("FH", 3072, 3200), ("y1", 3072, 3200), AF.Abs, 0.0, 0.5)
    dams1(tab, 0)
    act(("dmo", 0, 16), ("dmj", 0, 16), AF.Identity, 0.0, OWN)
    act(("dmh", 0, 16), ("dmj", 0, 16), AF.Identity, 0.0, HOWN)
    act(("i16", 0, 16), ("io", 0, 16), AF.Identity, 0.0, 0.0625)
    act(("nm", 0, 256), ("dmj", 0, 256), AF.Identity, 1.0e9, -1.0e9)
    ghosts1_act(1)
    ghosts1(1, tab)
    dams1(tab, 1)
    sires1(3)
    act((tab, Z0 + VD, Z0 + 3200), ("y1", VD, 3200), AF.Abs)
    dams1(tab, 2)
    dams1(tab, 3)
    REST = [(CUT + 512 * k, CUT + 512 * k + 512, pb) for k, pb in enumerate(("pA", "pB"))]
    HALF = [(0, CUT // 2), (CUT // 2, CUT)]
    copy(("sire16", 192, 384), ("sireI", 192, 384))
    copy(("dam16", 192, 384), ("damI", 192, 384))
    for a, b in HALF:
        act(("tmp", a, b), ((tab, Z0, OWN1), ("sire16", 192 + a // 16, 192 + b // 16)), AF.Identity)
    ghosts2_act(1, tab)
    for a, b, pb in REST:
        act(("tmp", a, b), ((tab, Z0, OWN1), ("sire16", 192 + a // 16, 192 + b // 16)), AF.Identity)
        mm((pb, 0, 512), ("ident", 0, 128), ("tmp", a, b), True, False)
    for a, b, pb in REST:
        act(("tmp2", a - CUT, b - CUT), ((tab, Z0, E1), ("dam16", 192 + a // 16, 192 + b // 16)), AF.Identity)
        mm((pb, 0, 512), ("ident", 0, 128), ("tmp2", a - CUT, b - CUT), False, True)
    copy(("CF", 1024, 2048), (("W", 0, WW), ("pos16", 64, 128)))
    dma("S", [(T.W[q:128:16, 8:WW], T.sire[:, 0:192]) for q in own[1:]], "l_w2", [], [("W", 8, WW)])
    for a, b in HALF:
        tt(("D2", a, b), ((tab, Z0, E1), ("dam16", 192 + a // 16, 192 + b // 16)), ("tmp", a, b), ALU.add)
    ghosts2(1, tab)
    u_lists(0)
    act(("T3", 0, 1024), ((tab, 0, E1), ("US16", 0, 64)), AF.Identity, KB)
    act(("T4", 0, KP), ((tab, Z0, X3), ("UD16", 0, KP // 16)), AF.Identity)
    mm(("pC", 0, KP), ("ident", 0, 128), ("T3", 0, KP), True, False)
    mm(("pC", 0, KP), ("ident", 0, 128), ("T4", 0, KP), False, True)
    JL, JB = [("cl", k, k + 1) for k in (0, 1)], [("cl", k, k + 1) for k in (2, 3)]
    scan(("tmp", 0, CUT), ("D2", 0, CUT), ("D2", 0, CUT), 0.0, ALU.max, ALU.max)
    scan(("FH", 0, CUT), ("D2", 0, CUT), ("D2", 0, CUT), 1.0e9, ALU.min, ALU.min)
    K, K2, LAST = ("cl", 8, 9), ("cl", 9, 10), ("tmp", 3071, 3072)
    for out, alu in (("tmp", ALU.max), ("FH", ALU.min)):
        for n, (a, b, pb) in enumerate(REST):
            scan((out, a, b), (pb, 0, 512), ("zero", 0, 512), (out, a - 1, a), alu, ALU.add)
            if out == "FH" and n == 0:
                act(("junk", 0, 192), ("tmp", 15, 3072, 16), AF.Sign, LAST, -1.0, K)
                ts(("off16", 0, 16), ("i16", 0, 16), K, ALU.add, 16.0, ALU.mult)
                tt(("mk", 0, 256), (("tmp", 0, 3072), ("off16", 0, 16)), ("nm", 0, 256), ALU.max)
                act(("junk", 0, 256), ("mk", 0, 256), AF.Sign, LAST, -1.0, K2)
    act(("seg", 512, 1024), ("io", 0, 512), AF.Sign)
    for k in (-1, 0, 1):
        act(("w3", 0, 128), ("Y", 0, 128), AF.Abs, float(-16 * k))
        for y, m, nm in ((0, Y0, NY0), (1, Y1, NY1)):
            if 0 <= y + k < 2:
                act(("R%d%d" % (y, y + k), 0, 128), ("w3", 0, 128), AF.Relu, m, nm)
    ts(JL[0], K, 16.0, ALU.mult, K2, ALU.add)
    act(("junk", 0, 3072), ("FH", 0, 3072), AF.Sign, ("FH", 3071, 3072), -1.0, JB[0])

    def founder_a(s, n):
        b = lambda k: ("cl", n + k, n + k + 1)
        ib = lambda k: ("ci", n + k, n + k + 1)
        ts(ib(0), s, -3200.0, ALU.add, 0.0, ALU.max)
        ts(b(0), s, 3200.0, ALU.is_lt, s, ALU.mult)
        ts(ib(1), ib(0), 15, ALU.bitwise_and)
        ts(b(1), ib(0), 0.0625, ALU.mult)
        ts(b(2), s, 3200.0, ALU.is_ge)
        ts(("sm16", n, n + 1), ib(1), 191.9375, ALU.mult, b(1), ALU.add)
        return ("sm16", n, n + 1)

    def founder_b(n):
        ts(("sm16", n + 2, n + 3), ("cl", n + 3, n + 4), ("cl", n + 2, n + 3), ALU.mult, ("cl", n, n + 1), ALU.add)
        return ("sm16", n + 2, n + 3)

    def chain1(land):
        J = JL[0]
        ts(("ci", 16, 17), J, 240.0, ALU.add)
        ts(("cl", 16, 17), J, 0.0625, ALU.mult, 15.0, ALU.add)
        ts(("ci", 17, 18), ("ci", 16, 17), 15, ALU.bitwise_and)
        ts(("sm16", 16, 17), ("ci", 17, 18), 191.9375, ALU.mult, ("cl", 16, 17), ALU.add)
        tt(("lk", 0, 16), (("trI", 0, 3072), ("sm16", 16, 17)), ("dmo", 0, 16), ALU.mult)
        red(("cl", 17, 18), ("lk", 0, 16))
        tt(("lk", 16, 32), (("W", 8, WW), founder_a(("cl", 17, 18), 20)), ("dmo", 0, 16), ALU.mult)
        red(("cl", 23, 24), ("lk", 16, 32))
        tt(("lk", 32, 48), (("y1", 0, 3072), founder_b(20)), ("dmh", 0, 16), ALU.mult)
        red((land, 4 * rank, 4 * rank + 1), ("lk", 32, 48))

    def best_lines_a():
        copy(("bg2", 0, 16), (("W", 8, WW), founder_a(("bsc", 15, 16), 32)))
        mm(("pM", 288, 304), ("bs1", 0, 128), ("bg2", 0, 16))

    def best_lines_b():
        tt(("bm2", 0, 16), ("pM", 288, 304), ("dmj", 0, 16), ALU.mult)
        red(("cl", 35, 36), ("bm2", 0, 16))
        copy(("yt16", 0, 16), (("y1", 0, 3072), founder_b(32)))

    def chain2(land):
        copy(("sm16", 40, 41), JL[1])
        tt(("lk", 48, 64), (("sy", 0, 1024), ("sm16", 40, 41)), ("dmh", 0, 16), ALU.mult)
        red((land, 4 * rank, 4 * rank + 1), ("lk", 48, 64))

    chain1("land1")
    share_aim("land1", "a_aim1")
    tt(("key", KP, 1024), ((tab, Z0, X3), ("UD16", KP // 16, 64)), ("T3", KP, 1024), ALU.add)

    def rows_a(k, between):
        turn(("D2", 1024 + k, 2048), ("key", k, 1024))
        if k:
            turn(("D2", 1024, 1024 + k), ("pC", 0, k))
        between()
        scan(("D2", 0, 1024), ("seg", 0, 1024), ("D2", 1024, 2048), 0.0, ALU.mult, ALU.max)

    def rows_b():
        ts(("ri", 0, 64), ("D2", 15, 1024, 16), 64.0, ALU.mult)
        ts(("rb", 0, 64), ("ri", 0, 64), 15, ALU.bitwise_and)
        copy(("rbf", 0, 64), ("rb", 0, 64))
        for y in range(2):
            for h in range(2):
                mm(("pM", 32 * y, 32 * y + 32), ("R%d%d" % (y, h), 0, 128), ("rbf", h, 64, 2), h == 0, h == 1)

    def rows_c(c0):
        for y in range(2):
            ts(("row16", c0 + y, c0 + 64, 2), ("pM", 32 * y, 32 * y + 32), -1.0, ALU.mult, 15.0, ALU.add)

    def best_a(r):
        k = 16 * (r - 1)
        ts(("bR", k, k + 16), ("dmj", 0, 16), JB[r - 1], ALU.mult, -1.0, ALU.mult)
        mm(("pY", 128 + k, 144 + k), ("blk", 0, 128), ("bR", k, k + 16))

    def best_b(r):
        k = 16 * (r - 1)
        copy(("bT", k, k + 16), ("pY", 128 + k, 144 + k))

    def sire_act(r, a=0, b=1024):
        k = 64 * (r - 1)
        act(("sf", 16 * k + a, 16 * k + b), (("bT", 16 * (r - 1), 16 * r), ("row16", k + a // 16, k + b // 16)), AF.Identity)

    def sire_cols(r):
        to_list("pE", "ZS", "sf", 1024 * (r - 1), 64 * (r - 1))

    BH = [("cl", 4, 5), ("cl", 5, 6)]

    def outputs(r, first):
        ts(("yso", 64 * (r - 1), 64 * r), ("pE", 64 * (r - 1), 64 * r), float(first), ALU.add)
        ts(("yto", r - 1, r), BH[r - 1], 2.0, ALU.mult, T1, ALU.add)

    def aims(r, land):
        op("V", lambda: g.vector.tensor_reduce(ap(BH[r - 1]), T[land][:, 0:16:4], AxisListType.X, ALU.add),
           [(land, 0, 16)], [BH[r - 1]])

    rows_a(KP, lambda: aims(1, "land1"))
    rows_b()
    n = 48
    best_a(1)
    copy(("ci", n, n + 1), JB[0])
    ts(("cl", n + 1, n + 2), JB[0], -0.0625, ALU.mult)
    ts(("ci", n + 2, n + 3), ("ci", n, n + 1), -1.0, ALU.mult)
    rows_c(0)
    ts(("ci", n + 1, n + 2), ("ci", n + 2, n + 3), 15, ALU.bitwise_and)
    ts(("sm16", n, n + 1), ("ci", n + 1, n + 2), 191.9375, ALU.mult, ("cl", n + 1, n + 2), ALU.add)
    copy(("bg", 0, 16), (("W", 8, WW), ("sm16", n, n + 1)))
    mm(("pM", 256, 272), ("bs2", 0, 128), ("bg", 0, 16))
    mm(("pM", 272, 288), ("bd2", 0, 128), ("bg", 0, 16))
    list_s(1)
    best_b(1)
    tt(("bm", 0, 32), ("pM", 256, 288), ("dmj", 0, 32), ALU.mult)
    scan(("bsc", 0, 32), ("seg", 0, 32), ("bm", 0, 32), 0.0, ALU.mult, ALU.add)
    copy(("sm16", n + 4, n + 8, 2), ("bsc", 15, 32, 16))
    BS, BD = ("sm16", n + 4, n + 5), ("sm16", n + 6, n + 7)

    def begin(r, tab):
        bias = BH[r - 2]
        for k in range(4):
            act(("FH", 800 * k, 800 * k + 800), ("y1", 800 * k, 800 * k + 800), AF.Abs, bias, -0.5)
        nv = 2 if r == 2 else 3
        for k in range(nv):
            ts((tab, Z0 + 800 * k, Z0 + 800 * k + 800), ("FH", 800 * k, 800 * k + 800), 2.0, ALU.mult)
        for k in range(4):
            sires1(k)
            dams1(tab, k)
            if k == 0:
                ghosts1_act(r)
                ghosts1(r, tab)
                if r == 2:
                    best_lines_a()
                    list_d(1)
        act((tab, Z0 + 800 * nv, Z0 + 3200), ("FH", 800 * nv, 3200), AF.Identity, 0.0, 2.0)
        if r == 3:
            sire_act(2, 0, 512)
        ghosts2_act(r, tab)
        copy(("ub1", 0, 16), ((tab, Z0, OWN1), BS))
        tt(("Ub", 0, 16), ((tab, Z0, E1), BD), ("ub1", 0, 16), ALU.add)
        ghosts2(r, tab)
        if r == 2:
            best_lines_b()
        else:
            outputs(1, 6400)
        for k in range(2):
            a, b = 512 * k, 512 * k + 512
            act(("tmp2", a, b), (("Ub", 0, 16), ("row16", 32 * k, 32 * k + 32)), AF.Identity)
            tt(("T3", a, b), ((tab, 0, E1), ("US16", 32 * k, 32 * k + 32)), ("tmp2", a, b), ALU.add)
        if r == 2:
            u_lists(1)
            act(("sy", 0, 1024), (("yt16", 0, 16), ("row16", 0, 64)), AF.Identity)
        else:
            sire_act(2, 512, 1024)
            sire_cols(2)
        act(("T4", 0, 1024), ((tab, 0, E1), ("US16", 64, 128)), AF.Identity, KB if r == 2 else 0.0)
        tt(("G3", 0, 1024), ((tab, Z0, X3), ("UD16", 0, 64)), ("T3", 0, 1024), ALU.add)

    tab = "tabB"
    begin(2, tab)
    ghosts3(2, tab)
    scan(("tmp", 0, 1024), ("G3", 0, 1024), ("G3", 0, 1024), 0.0, ALU.max, ALU.max)
    double3(tab)
    act(("junk", 0, 1024), ("tmp", 0, 1024), AF.Sign, ("tmp", 1023, 1024), -1.0, JL[1])
    scan(("FH", 0, 1024), ("G3", 0, 1024), ("G3", 0, 1024), 1.0e9, ALU.min, ALU.min)
    act(("junk", 0, 1024), ("FH", 0, 1024), AF.Sign, ("FH", 1023, 1024), -1.0, JB[1])
    sire_act(1)
    chain2("land2")
    share_aim("land2", "a_aim2")
    tt(("key", 0, 1024), ((tab, Z0, TW), ("UD16", 64, 128)), ("T4", 0, 1024), ALU.add)
    rows_a(0, lambda: aims(2, "land2"))
    rows_b()
    best_a(2)
    sire_cols(1)
    ts(("sm16", 58, 59), JB[1], -1.0, ALU.mult)
    rows_c(64)
    best_b(2)

    tab = "tabA"
    begin(3, tab)
    double3(tab)
    ghosts3(3, tab)
    ts(("HB", 0, 16), (("G3", 0, 1024), ("sm16", 58, 59)), 0.5, ALU.mult)
    tt(("T3", 0, 1024), (("HB", 0, 16), ("row16", 64, 128)), ("T4", 0, 1024), ALU.add)
    act(("yo", 0, 1024), ("G3", 0, 1024), AF.Identity, 65535.0, -0.25)
    dma("S", [(T.yf[:, 0:1024], T.yo[:, 0:1024])], "o_f3", [("yo", 0, 1024)], [])
    b = 0
    for k, n in enumerate((384, 384, 256)):
        a, b = b, b + n
        tt(("key", a, b), ((tab, Z0, TW), ("UD16", 64 + a // 16, 64 + b // 16)), ("T3", a, b), ALU.add)
        act(("yo", 1024 + a, 1024 + b), ("key", a, b), AF.Identity, 65535.0, -0.25)
        dma("S", [(T.yf[:, 1024 + a:1024 + b], T.yo[:, 1024 + a:1024 + b])], "o_f4%s" % "abc"[k], [("yo", 1024 + a, 1024 + b)], [])
        if k == 1:
            outputs(2, 9600)
            dma("S", [(T.ys[:], T.yso[:])], "o_ys", [("yso", 0, 128)], [])
            dma("S", [(T.yt[:], T.yto[:])], "o_yt", [("yto", 0, 2)], [])

    for s in sorted(total):
        if known["G"].get(s, 0) < total[s]:
            g.wait_ge(T.sem[s], total[s])
    g.wait_ge(T.sem.sent, sent[0])
